import numpy as np, ml_dtypes
CORES = [16,18,20,22]
N = 4
BF = ml_dtypes.bfloat16
W, I, S, JU, RO = 4096, 1024, 8, 8, 2
def pick(a, ix):
    return np.take_along_axis(a, ix, 2) if a.ndim == 3 else np.take_along_axis(a, ix[:, :, None, :], 3)
def walk(u, par, side, heads):
    w = heads; c = heads; acc = np.zeros((N, 8, 16, I), np.int64)
    for _ in range(S):
        v = pick(u, w); up = np.add.reduce((v >= 4).astype(np.int64), axis=2) >= 9
        acc = acc + np.where(up[:, :, None, :], v, 0)
        sd = pick(side, c); w = np.where(up, pick(par, w), sd); c = np.where(up, c, sd)
    return acc
def forest(rng, alike, noise, ex):
    par = np.zeros((N, 8, W), np.int64); side = np.zeros((N, 8, W), np.int64); itm = np.zeros((N, 8, W), np.int64); bit = np.zeros((N, 8, W), np.int64); heads = np.zeros((N, 8, I), np.int64)
    pop = [rng.permutation(I) for g in range(8)]; n = np.arange(W); m = np.arange(W - 1)
    for q in range(N):
        for g in range(8):
            it = pop[g][np.minimum((I * rng.random(W) ** ex).astype(np.int64), I - 1)]; itm[q, g] = it
            o = np.argsort(it[1:], kind="stable") + 1; k = it[o]
            new = np.concatenate([np.array([True]), k[1:] != k[:-1]])
            side[q, g, o[:-1]] = np.where(new[1:], 0, o[1:]); heads[q, g, k[new]] = o[new]
            base = np.maximum(np.minimum((n * rng.random(W) ** 0.4).astype(np.int64), n - 1), 0)
            run = np.maximum.accumulate(np.where(new | (rng.random(W - 1) >= alike), m, 0))
            par[q, g, o] = base[o[run]]
            bit[q, g, o] = (m + (rng.random(W - 1) < noise)) & 1
    return par, side, itm, bit, heads
def counts(rng, e):
    lev = rng.random((N, 8, 1, W)) ** e
    u = np.where(rng.random((N, 8, 16, W)) < lev, rng.integers(4, 16, (N, 8, 16, W)), rng.integers(0, 4, (N, 8, 16, W)))
    u[..., 0] = 0
    return u
def level(u, par, side, heads, share):
    s = np.sort(np.add.reduce(walk(u, par, side, heads), axis=0), axis=2)
    j = np.minimum((I * share).astype(np.int64), I - 1)
    return np.clip(s[np.arange(8)[:, None], np.arange(16)[None, :], j[:, None]], 1, 1024)
def pack(u, par, side, itm, bit, heads, th):
    return {"cnt": np.ascontiguousarray(u.reshape(N, 128, W)).astype(np.float32).astype(BF), "par": par.astype(np.int32), "side": side.astype(np.int32), "itm": itm.astype(np.int32),
            "bit": bit.astype(np.int32), "heads": heads.astype(np.int32), "th": np.repeat(th.reshape(1, 128, 1), N, axis=0).astype(np.int32)}
def setup_inputs(rng):
    par, side, itm, bit, heads = forest(rng, 0.5, 0.25, 2.0); u = counts(rng, 0.5)
    return pack(u, par, side, itm, bit, heads, level(u, par, side, heads, 0.35 + 0.4 * rng.random(8)))
def setup_inputs_ties(rng):
    par, side, itm, bit, heads = forest(rng, 0.5, 0.25, 2.0)
    r = np.argsort(rng.random((N, 8, 16, W)), axis=2); m = 8 + (rng.random((N, 8, 1, W)) < 0.7)
    u = np.where(r < m, np.where(rng.random(r.shape) < 0.8, 4, rng.integers(4, 16, r.shape)), 3); u[..., 0] = 0
    tot = np.add.reduce(walk(u, par, side, heads), axis=0)
    i0 = np.argsort(np.min(tot, axis=1), axis=1, kind="stable")[:, I // 2]
    x = np.stack([tot[g, :, i0[g]] for g in range(8)]); k = np.argsort(rng.random((8, 16)), axis=1)
    th = np.where(k < 8 + (np.arange(8)[:, None] & 1), x, x + 1)
    return pack(u, par, side, itm, bit, heads, np.clip(th, 1, 1024))
def setup_inputs_deep(rng):
    par, side, itm, bit, heads = forest(rng, 0.5, 0.25, 2.0); u = counts(rng, 0.5); n = np.arange(W)
    par[:, 0::2] = np.maximum(n - 1, 0); par[:, 1::2] = np.maximum(n - 1 - rng.integers(0, 3, (N, 4, W)), 0)
    u = np.where(rng.random((N, 8, 1, W)) < 0.15, 15, u); u[..., 0] = 0
    th = level(u, par, side, heads, np.array([0.8, 0.9, 0.7, 0.5, 0.5, 0.5, 0.95, 0.6]))
    th[3] = 1024; th[4] = 1
    return pack(u, par, side, itm, bit, heads, th)
def one_chain(rng, par, side, itm, bit, heads, u):
    for q in range(N):
        for g in range(4):
            o = np.concatenate([np.array([W - 1]), rng.permutation(W - 2) + 1]); top = o[1]
            side[q, g] = 0; side[q, g, o[:-1]] = o[1:]
            if g == 1: side[q, g, o[1::2]] = 0
            bit[q, g, o] = (np.arange(W - 1) + (g == 1)) & 1
            par[q, g] = top; par[q, g, 0] = 0
            itm[q, g] = rng.integers(0, I, W); itm[q, g, top] = 0
            heads[q, g] = rng.integers(1, W, I); heads[q, g, 0] = top
            u[q, g] = rng.integers(4, 16, (16, W)); u[q, g, :, top] = rng.integers(12, 16, 16); u[q, g, :, 0] = 0
def setup_inputs_merge(rng):
    par, side, itm, bit, heads = forest(rng, 0.9, 0.5, 3.0); u = counts(rng, 0.4)
    one_chain(rng, par, side, itm, bit, heads, u)
    th = level(u, par, side, heads, 0.03 + 0.17 * rng.random(8))
    tot = np.add.reduce(walk(u, par, side, heads), axis=0)
    th[:2] = np.min(tot[:2], axis=2)
    th[2] = np.sort(tot[2], axis=1)[:, I // 2] | 1
    i0 = np.argsort(np.add.reduce(tot[3], axis=0), kind="stable")[I // 2]; k = np.argsort(rng.random(16))
    th[3] = np.where(k < 9, tot[3, :, i0], tot[3, :, i0] + 1)
    return pack(u, par, side, itm, bit, heads, th)
def setup_inputs_wild(rng):
    par = rng.integers(0, W, (N, 8, W)); itm = rng.integers(0, I, (N, 8, W)); bit = rng.integers(0, 2, (N, 8, W)); side = np.zeros((N, 8, W), np.int64)
    par[..., 1] = W - 1; zz = np.zeros((N, 8), np.int64)
    for q in range(N):
        for g in range(8):
            o = rng.permutation(W - 1) + 1; x, y, z, rest = o[:32], o[32:64], o[64], o[65:]
            a, b = rng.permutation(rest), rng.permutation(rest); h = W - W // 5
            side[q, g, a[:h]] = b[:h]; side[q, g, x] = y; side[q, g, y] = x; side[q, g, z] = z; zz[q, g] = z; bit[q, g, x] = 0; bit[q, g, y] = 1
            sel = np.nonzero((side[q, g] > 0) & (rng.random(W) < 0.6))[0]; p = par[q, g].copy(); p[side[q, g, sel]] = par[q, g, sel]; p[y] = p[x]; p[z] = 0; par[q, g] = p
    par[..., 0] = 0
    heads = np.where(rng.random((N, 8, I)) < 0.3, rng.choice(np.array([0, 1, W - 1]), (N, 8, I)), rng.integers(0, W, (N, 8, I)))
    heads[:, 0] = rng.choice(np.array([1, W - 1, W // 2, 5]), (N, I))
    heads[:, :, 3] = zz
    u = counts(rng, 0.5); u[np.arange(N)[:, None], np.arange(8)[None, :], :, zz] = 15
    return pack(u, par, side, itm, bit, heads, level(u, par, side, heads, 0.3 + 0.3 * rng.random(8)))
def setup_inputs_spread(rng):
    par, side, itm, bit, heads = forest(rng, rng.random(), 0.3, 4.0)
    u = np.minimum((16 * rng.random((N, 8, 16, W)) ** np.exp2(rng.integers(-3, 3, (N, 8, 1, W)))).astype(np.int64), 15)
    u = np.where(rng.random((N, 8, 1, W)) < 0.0625, 0, u); u[..., 0] = 0
    return pack(u, par, side, itm, bit, heads, level(u, par, side, heads, rng.permutation(np.array([0.02, 0.15, 0.3, 0.45, 0.55, 0.7, 0.85, 0.97]))))
def check_inputs(d):
    bad = []
    for k, lo, hi in (("par", 0, W - 1), ("side", 0, W - 1), ("itm", 0, I - 1), ("bit", 0, 1), ("heads", 0, W - 1), ("th", 1, 1024)):
        if np.min(d[k]) < lo or np.max(d[k]) > hi: bad.append("range of " + k)
    c = d["cnt"].astype(np.float32)
    if not np.all((c >= 0) & (c <= 15) & (c == np.floor(c))): bad.append("cnt: whole numbers from 0 to 15")
    if np.any(c[:, :, 0] != 0): bad.append("cnt of node 0")
    for k in ("par", "side"):
        if np.any(d[k][:, :, 0] != 0): bad.append(k + " of node 0")
    s = np.sort(d["side"], axis=2)
    if np.any((s[:, :, 1:] == s[:, :, :-1]) & (s[:, :, 1:] != 0)): bad.append("side: numbers other than 0 differ")
    if np.any(d["th"] != d["th"][:1]): bad.append("th alike on all ranks")
    return bad
def reference(cnt, par, side, itm, bit, heads, th):
    u = cnt.astype(np.float32).astype(np.int64).reshape(N, 8, 16, W); pa = par.astype(np.int64); sd = side.astype(np.int64)
    it = itm.astype(np.int64); b = bit.astype(np.int64); hd = heads.astype(np.int64); lim = th[0].astype(np.int64).reshape(8, 16, 1)
    node = np.broadcast_to(np.arange(W), (N, 8, W)); own = []
    for t in range(RO):
        tot = np.add.reduce(walk(u, pa, sd, hd), axis=0)
        own.append(np.stack([tot[:, :, r * (I // N):(r + 1) * (I // N)].reshape(128, I // N) for r in range(N)]))
        kept = np.add.reduce((tot >= lim).astype(np.int64), axis=1) >= 9
        kn = pick(np.broadcast_to(kept[None], (N, 8, I)), it); kn[:, :, 0] = True
        jump = np.where(kn, node, pa); p1 = pa
        for _ in range(JU): p1 = pick(jump, p1)
        u1 = np.where(pick(kn, pa)[:, :, None, :], u, np.minimum(15, u + pick(u, pa)))
        ab = kn & (sd != 0) & (p1 == pick(p1, sd)) & (b == t % 2) & (pick(b, sd) == 1 - t % 2)
        u = np.where(ab[:, :, None, :], np.minimum(15, u1 + pick(u1, sd)), u1)
        rep = np.array(node); a, g, n = np.nonzero(ab); rep[a, g, sd[a, g, n]] = n
        sd = np.where(ab, pick(sd, sd), np.where(rep != node, 0, sd))
        pa = pick(rep, p1)
    return {"ya": np.concatenate(own, axis=2).astype(np.float32), "yc": np.ascontiguousarray(u.reshape(N, 128, W)).astype(np.float32).astype(BF), "yp": pa.astype(np.float32)}

@@ -1,0 +1,662 @@
+from concourse.bass import DstId, RemoteDMATransfer
+from concourse.mybir import AluOpType, ActivationFunctionType
+
+W, NI, STEPS, ROUNDS = 4096, 1024, 8, 2
+ZW = 144
+ZN = ["A", "B", "C", "PAR", "SD", "IT", "J", "KP", "PO", "PP", "PS", "NN", "BIT", "R1", "R9"]
+PRM = dict(iv=512, uv=(320, 512), kv0=12, gs=2048, pav=(0, 1024), lv=((60, 60, 40), (64, 64, 60)), ppv=(64, 64),
+           sc_step=128, sc_w=3328, sc_lv=128, pre=(4096, 3072))
+
+BF, F32, I32, U16 = "bfloat16", "float32", "int32", "uint16"
+SCRATCH = {
+    "UU": ("sbuf", [128, 2 * W], BF), "U1": ("sbuf", [128, W], BF), "TT": ("sbuf", [128, W], BF),
+    "WT": ("sbuf", [128, 2 * W], BF), "INV": ("sbuf", [128, 2 * W], BF), "D": ("sbuf", [128, W], BF),
+    "X0": ("sbuf", [128, W], BF), "J2": ("sbuf", [128, W], BF), "J4": ("sbuf", [128, W], BF),
+    "J8": ("sbuf", [128, W], BF), "P1": ("sbuf", [128, W], BF), "PPB": ("sbuf", [128, W], BF),
+    "KPB": ("sbuf", [128, W], BF),
+    "REPF": ("sbuf", [128, W], F32), "PAO": ("sbuf", [128, W], F32),
+    "GI0": ("sbuf", [128, NI], BF), "GI1": ("sbuf", [128, NI], BF),
+    "GU0": ("sbuf", [128, NI], BF), "GU1": ("sbuf", [128, NI], BF),
+    "ACC": ("sbuf", [128, NI], BF), "K0": ("sbuf", [128, NI], BF), "K1": ("sbuf", [128, NI], BF),
+    "LAND0": ("sbuf", [128, NI], BF), "LAND1": ("sbuf", [128, NI], BF),
+    "VI": ("sbuf", [128, 256], BF), "VK": ("sbuf", [128, 256], BF), "YA": ("sbuf", [128, 512], F32),
+    "INI": ("sbuf", [128, 1088], I32), "HI": ("sbuf", [128, 576], I32), "LO": ("sbuf", [128, 576], I32),
+    "HB": ("sbuf", [128, 1088], BF), "LB": ("sbuf", [128, 1088], BF),
+    "BI": ("sbuf", [128, 256], I32), "BITB": ("sbuf", [128, 256], BF), "NBIT": ("sbuf", [128, 256], BF),
+    "BROW": ("sbuf", [128, 256], BF), "RB2": ("sbuf", [128, 512], BF), "M": ("sbuf", [128, 256], BF),
+    "W2": ("sbuf", [128, 512], BF), "AB": ("sbuf", [128, 256], BF), "VB": ("sbuf", [128, 256], BF),
+    "NBF": ("sbuf", [128, 256], F32), "RBF": ("sbuf", [128, 256], F32), "WF": ("sbuf", [128, 256], F32),
+    "NI4": ("sbuf", [128, 256], F32), "FA": ("sbuf", [128, 256], F32), "FB": ("sbuf", [128, 256], F32),
+    "FC": ("sbuf", [128, 256], F32), "FD": ("sbuf", [128, 256], F32), "SIDE": ("sbuf", [128, 256], F32),
+    "SA0": ("sbuf", [128, 256], F32), "SA1": ("sbuf", [128, 256], F32), "BIF": ("sbuf", [128, 256], F32),
+    "BV": ("sbuf", [128, 256], F32),
+    "SCO": ("sbuf", [128, 256], U16), "PARI": ("sbuf", [128, 256], U16), "ITI": ("sbuf", [128, 256], U16),
+    "IPO": ("sbuf", [128, 256], U16), "PDO": ("sbuf", [128, 256], U16), "JO0": ("sbuf", [128, 256], U16),
+    "JO1": ("sbuf", [128, 256], U16), "PT0": ("sbuf", [128, 256], U16), "PT1": ("sbuf", [128, 256], U16),
+    "GO": ("sbuf", [128, 256], U16), "P1O": ("sbuf", [128, 256], U16),
+    "OFF0": ("sbuf", [128, 64], U16), "OFF": ("sbuf", [128, 512], U16), "OC": ("sbuf", [128, 512], U16),
+    "Q0": ("sbuf", [128, 64], F32), "Q": ("sbuf", [128, 64], F32), "OFFF": ("sbuf", [128, 128], F32),
+    "ZS": ("sbuf", [128, ZW * len(ZN)], BF), "Z1": ("sbuf", [128, ZW], BF), "ONE": ("sbuf", [128, 128], BF),
+    "BO": ("sbuf", [128, 128], BF), "IDN": ("sbuf", [128, 128], BF), "IDF": ("sbuf", [128, 128], F32),
+    "RI": ("sbuf", [128, 8], I32), "RJ": ("sbuf", [128, 8], I32), "RF": ("sbuf", [128, 8], F32),
+    "IO16": ("sbuf", [128, 16], F32), "OH": ("sbuf", [128, 16], F32), "OP": ("sbuf", [128, 8], F32),
+    "CF": ("sbuf", [128, 16], F32), "THI": ("sbuf", [128, 4], I32), "THF": ("sbuf", [128, 4], F32),
+}
+for _b in range(8):
+    SCRATCH["ps%d" % _b] = ("psum", [128, 512], F32)
+NDS = 70
+SEMAPHORES = ["cV", "cS", "cP", "cG", "la0", "la1", "ka0", "ka1", "l0", "l1", "l2", "l3"] + ["d%d" % _i for _i in range(NDS)]
+ESZ = {BF: 2, F32: 4, I32: 4, U16: 2}
+
+
+def rank_program(g, core, T, topo):
+    rank = T.rank_of(core)
+    if rank is None:
+        return
+    P = PRM
+    NR = len(T.cores)
+    OWN = NI // NR
+    op = AluOpType
+    fn = ActivationFunctionType
+    eng = {"V": g.vector, "S": g.scalar, "P": g.tensor, "G": g, "Y": g.sync}
+    count = {}
+    waited = {e: {} for e in eng}
+    hist = {}
+    nds = [0]
+
+    def A(name, a=None, b=None, step=1, row=None, rs=16):
+        wd = SCRATCH[name][1][1]
+        a = 0 if a is None else a
+        b = wd if b is None else b
+        es = ESZ[SCRATCH[name][2]]
+        if SCRATCH[name][0] == "psum":
+            reg = (name, 0xFFFF, 0, 2048)
+        else:
+            m = 0xFFFF if row is None else sum(1 << r for r in range(row, 16, rs))
+            reg = (name, m, a * es, b * es)
+        ps = slice(None) if row is None else slice(row, None, rs)
+        cs = slice(a, b) if step == 1 else slice(a, b, step)
+        return (T[name][ps, cs], [reg])
+
+    def IX(win, off):
+        return (win[0].indirect(off[0]), win[1] + off[1])
+
+    def wait(e, sem, val):
+        if waited[e].get(sem, 0) < val:
+            eng[e].wait_ge(T.sem[sem], val)
+            waited[e][sem] = val
+
+    def sync(e, who, reads, writes):
+        need = {}
+        for rg, wr in ((reads, False), (writes, True)):
+            for (nm, m, lo, hi) in rg:
+                psum = nm.startswith("ps")
+                for (m2, lo2, hi2, who2, tok, wr2) in hist.get(nm, []):
+                    if not (m & m2) or hi <= lo2 or hi2 <= lo:
+                        continue
+                    if psum:
+                        hit = who != who2
+                    else:
+                        hit = wr or wr2
+                    if hit:
+                        need[tok[0]] = max(need.get(tok[0], 0), tok[1])
+        for s in sorted(need):
+            wait(e, s, need[s])
+
+    def note(who, tok, reads, writes):
+        for rg, wr in ((reads, False), (writes, True)):
+            for (nm, m, lo, hi) in rg:
+                h = hist.setdefault(nm, [])
+                if wr or nm.startswith("ps"):
+                    h[:] = [x for x in h if not ((x[0] & ~m) == 0 and lo <= x[1] and x[2] <= hi)]
+                else:
+                    h[:] = [x for x in h if not (who is not None and x[3] == who and not x[5]
+                                                 and (x[0] & ~m) == 0 and lo <= x[1] and x[2] <= hi)]
+                h.append((m, lo, hi, who, tok, wr))
+
+    def regs(xs):
+        return [r for x in xs if isinstance(x, tuple) for r in x[1]]
+
+    def raw(x):
+        return x[0] if isinstance(x, tuple) else x
+
+    def comp(e, call, outs, ins, offs=()):
+        sync(e, e, regs(ins) + list(offs), regs(outs))
+        s = "c" + e
+        count[s] = count.get(s, 0) + 1
+        call().then_inc(T.sem[s], 1)
+        note(e, (s, count[s]), regs(ins) + list(offs), regs(outs))
+
+    def copy(o, i):
+        comp("V", lambda: g.vector.tensor_copy(o[0], i[0]), [o], [i])
+
+    def tt(o, a, b, f):
+        comp("V", lambda: g.vector.tensor_tensor(o[0], a[0], b[0], f), [o], [a, b])
+
+    def ts(o, a, s1, f0, s2=None, f1=None):
+        if f1 is None:
+            comp("V", lambda: g.vector.tensor_scalar(o[0], a[0], raw(s1), None, f0), [o], [a, s1])
+        else:
+            comp("V", lambda: g.vector.tensor_scalar(o[0], a[0], raw(s1), raw(s2), f0, f1), [o], [a, s1, s2])
+
+    def memset(o, v):
+        comp("V", lambda: g.vector.memset(o[0], v), [o], [])
+
+    def act(o, i, f=fn.Copy, bias=None, scale=None):
+        if bias is not None and scale is not None:
+            comp("S", lambda: g.scalar.activation(o[0], i[0], f, bias=raw(bias), scale=raw(scale)), [o], [i, bias, scale])
+        elif bias is not None:
+            comp("S", lambda: g.scalar.activation(o[0], i[0], f, bias=raw(bias)), [o], [i, bias])
+        elif scale is not None:
+            comp("S", lambda: g.scalar.activation(o[0], i[0], f, scale=raw(scale)), [o], [i, scale])
+        else:
+            comp("S", lambda: g.scalar.activation(o[0], i[0], f), [o], [i])
+
+    def iota(o, pat, base, cm, flt=True):
+        if flt:
+            comp("G", lambda: g.iota(o[0], pat, base, cm, allow_small_or_imprecise_dtypes=True), [o], [])
+        else:
+            comp("G", lambda: g.iota(o[0], pat, base, cm), [o], [])
+
+    def asel(o, i, pat, cmp, base, cm):
+        comp("G", lambda: g.affine_select(o[0], i[0], pat, cmp, 0.0, base, cm), [o], [i])
+
+    def mms(o, terms, start, stop):
+        ins = [x for t in terms for x in t]
+        sync("P", "P", regs(ins), regs([o]))
+        count["cP"] = count.get("cP", 0) + 1
+        for k, (l, r) in enumerate(terms):
+            h = g.tensor.matmul(o[0], l[0], r[0], start and k == 0, stop and k == len(terms) - 1)
+        h.then_inc(T.sem["cP"], 1)
+        note("P", ("cP", count["cP"]), regs(ins), regs([o]))
+
+    def Z(z, i):
+        if z == "ONE":
+            return A("Z1", 15 - i, 143 - i)
+        o = ZN.index(z) * ZW
+        return A("ZS", o + 15 - i, o + 143 - i)
+
+    def wrap(o, z, src, a, b, start=True, stop=True, more=()):
+        mms(o, [(Z(z, i), A(src, a + i, b, 16)) for i in range(16)] + list(more), start, stop)
+
+    def block(o, z, src, q0, q1, start=True, stop=True):
+        mms(o, [(Z(z, i), A(src, 256 * i, 256 * i + 256)) for i in range(q0, q1)], start, stop)
+
+    def dma(e, pairs, add=False, slow=False):
+        s = "d%d" % nds[0]
+        nds[0] += 1
+        sync(e, None, regs([p[1] for p in pairs]), regs([p[0] for p in pairs]))
+        for o, i in pairs:
+            if add:
+                h = g.dma_start(raw(o), raw(i), accum_op=op.add)
+            elif slow:
+                h = g.dma_start(raw(o), raw(i), allow_slow_non_contiguous=True)
+            else:
+                h = eng[e].dma_start(raw(o), raw(i))
+            h.then_inc(T.sem[s], 16)
+        count[s] = 16 * len(pairs)
+        note(None, (s, count[s]), regs([p[1] for p in pairs]), regs([p[0] for p in pairs]))
+
+    peers = [c for c in T.cores if c != core]
+    peers.sort(key=lambda c: topo.die(c) == topo.die(core))
+    lanes = (0, 2, 1)
+
+    def exchange(src_of, dst, land, rsem, lsem):
+        trs, reads, ne = [], [], 0
+        for k, c in enumerate(peers):
+            es = topo.engines(core, c)[lanes[k]::4]
+            rid, pid, _ = topo.addr(c)
+            s = src_of(T.rank_of(c))
+            reads.append(s)
+            ne += len(es)
+            trs.append(RemoteDMATransfer(dst_ids=[DstId(rid=rid, pnc=pid)], dma_engine_mask=sum(1 << x for x in es),
+                                         remote_sem=T.sem[rsem], src=s[0], dst=dst[0]))
+        sync("G", None, regs(reads), [])
+        g.remote_dma_fused(trs, local_sem=T.sem[lsem])
+        count[lsem] = ne
+        note(None, (lsem, ne), regs(reads), [])
+        count[rsem] = sum(len(topo.engines(c, core)[0::4]) for c in peers)
+        note(None, (rsem, count[rsem]), [], regs(land))
+
+    def col(name, j):
+        return A(name, j, j + 1)
+
+    def ps(b, a=0, e=256):
+        return A("ps%d" % b, a, e)
+
+    FR = W
+    H = W // 2
+    NN_, PA_, SD_, HD_, IT_ = 0, 256, 512, 768, 832
+    CA, CB, CC, CJ, CD, CPO, CPE, CPP, CPS, CKP, CKS, CKB, CT0, CT1, CX = range(15)
+
+    def rows(dst, r, a, src_off, n=256, wd=W):
+        return [(A(dst, a, a + wd, row=r), A("HB", src_off, src_off + n)),
+                (A(dst, a, a + wd, row=r + 8), A("LB", src_off, src_off + n))]
+
+    def split_bits(a, b):
+        ts(A("HI", 0, b - a), A("INI", a, b), 4032, op.bitwise_and)
+        ts(A("LO", 0, b - a), A("INI", a, b), 63, op.bitwise_and)
+
+    def split_cast(a, b):
+        copy(A("HB", a, b), A("HI", 0, b - a))
+        copy(A("LB", a, b), A("LO", 0, b - a))
+
+    def split(a, b):
+        split_bits(a, b)
+        split_cast(a, b)
+
+    sc_done = [0]
+
+    def scatter(n):
+        a = sc_done[0]
+        n = min(n, W - a)
+        if n > 0:
+            off = A("SCO", a // 16, (a + n) // 16)
+            src = A("WT", FR + a, FR + a + n)
+            comp("V", lambda: g.vector.tensor_copy(IX(A("INV"), off)[0], src[0]), [A("INV")], [src], off[1])
+            sc_done[0] = a + n
+
+    def sign_v(src, a, b):
+        ts(A("X0", a, b), src, 3.5, op.is_ge)
+
+    def sign_s(src, a, b):
+        act(A("X0", a, b), src, fn.Sign, bias=col("CF", CX))
+
+    def climb_rows(ct):
+        ts(A("VB"), ps(7), col("CF", ct), op.subtract, 1.0, op.is_lt)
+        dma("Y", [(A("WT", FR, FR + W, row=14), A("VB"))])
+
+    dma("Y", [(A("INI", PA_, PA_ + 256), T.par[:]), (A("INI", SD_, SD_ + 256), T.side[:]),
+              (A("INI", HD_, HD_ + 64), T.heads[:])])
+    for k in range(4):
+        dma("Y", [(A("UU", 1024 * k, 1024 * k + 1024), T.cnt[:, 1024 * k:1024 * k + 1024])])
+    iota(A("INI", NN_, NN_ + 256), [[1, 256]], 0, 256, False)
+    iota(col("RI", 0), [[0, 1]], 0, 1, False)
+    iota(A("IO16"), [[1, 16]], 0, 0)
+    iota(A("ONE"), [[0, 128]], 1, 0)
+    iota(A("Z1"), [[0, ZW]], 0, 0)
+    asel(A("Z1", 15, 128, 16), A("ONE", 0, 8), [[-16, 8]], op.is_ge, 0, 1)
+    asel(A("Z1", 15, 128, 16), A("Z1", 15, 128, 16), [[16, 8]], op.is_ge, 15, -1)
+    asel(A("IDN"), A("ONE"), [[-1, 128]], op.is_equal, 0, 1)
+    iota(A("WT", 0, W), [[0, W]], 0, 0)
+    iota(A("NI4"), [[16, 256]], W, 0)
+    dma("G", [(col("THI", 0), T.th[:])], slow=True)
+    iota(A("D"), [[0, W]], 0, 0)
+    iota(A("INV", 0, W), [[0, W]], 0, 0)
+    asel(A("BO"), A("ONE"), [[-16, 8], [0, 16]], op.is_ge, 0, 1)
+    asel(A("BO"), A("BO"), [[16, 8], [0, 16]], op.is_ge, 15, -1)
+
+    memset(A("WT", FR, FR + W), 1.0)
+    memset(col("CF", CX), -3.5)
+    ts(col("RJ", 0), col("RI", 0), 15, op.bitwise_and)
+    ts(col("RJ", 1), col("RI", 0), 7, op.bitwise_and)
+    split(NN_, NN_ + 256)
+    dma("S", rows("WT", 1, FR, NN_))
+    copy(A("RF", 0, 2), A("RJ", 0, 2))
+    memset(A("GI1"), 0.0)
+    ts(A("OH"), A("IO16"), col("RF", 0), op.is_equal)
+    ts(A("OP"), A("IO16", 0, 8), col("RF", 1), op.is_equal)
+    split(PA_, IT_)
+    dma("Y", rows("GI1", 0, 0, HD_, 64, NI))
+    dma("Y", rows("WT", 2, FR, SD_) + rows("WT", 0, FR, PA_))
+    ts(col("CF", CT0), col("RF", 0), float(P["kv0"]), op.is_ge, 7.5, op.mult)
+    ts(col("CF", CA), col("OH", 14), 8192.0, op.mult, col("OP", 0), op.add)
+    ts(col("CF", CB), col("OP", 2), col("OP", 1), op.subtract)
+    ts(col("CF", CC), col("OH", 14), 2.0, op.mult, col("OH", 15), op.add)
+    ts(col("CF", CJ), col("OP", 0), col("OP", 1), op.add)
+    ts(col("CF", CD), col("OP", 3), col("OP", 4), op.add)
+    ts(col("CF", CPE), col("OH", 6), 8.0, op.mult, col("OP", 7), op.add)
+    ts(col("CF", CKP), col("OH", 1), -4096.0, op.mult)
+    ts(col("CF", CKS), col("OP", 1), col("OP", 4), op.add)
+    ts(col("CF", CKB), col("OP", 2), col("OH", 6), op.add, col("OH", 15), op.add)
+    ts(col("CF", CT1), col("RF", 0), float(P["gs"] // 256), op.is_ge, 7.5, op.mult)
+    ts(col("CF", CC), col("CF", CC), -4096.0, op.mult)
+    ts(col("CF", CPO), col("CF", CJ), col("CF", CD), op.subtract)
+    ts(col("CF", CKS), col("CF", CKS), 2.0, op.mult, -1.0, op.add)
+    ts(col("CF", CPP), col("CF", CPE), 8192.0, op.mult, col("CF", CPO), op.add)
+    ts(col("CF", CPS), col("CF", CPE), 8192.0, op.mult, col("CF", CPO), op.subtract)
+    ts(col("CF", CKB), col("CF", CKB), 100.0, op.mult, col("CF", CKS), op.subtract)
+    zcol = {"A": col("CF", CA), "B": col("CF", CB), "C": col("CF", CC), "PAR": col("OP", 0),
+            "SD": col("OP", 2), "IT": col("OP", 5), "J": col("CF", CJ), "KP": col("CF", CKP), "PO": col("CF", CPO),
+            "PP": col("CF", CPP), "PS": col("CF", CPS), "NN": col("OP", 1), "BIT": col("OH", 6),
+            "R1": col("OH", 1), "R9": col("OH", 9)}
+
+    def zmake(names):
+        for z in names:
+            o = ZN.index(z) * ZW
+            act(A("ZS", o, o + ZW), A("Z1"), fn.Copy, scale=zcol[z])
+
+    kv = 256 * P["kv0"]
+    zmake(["PAR", "SD"])
+    act(A("IDF"), A("IDN"))
+    for k in range(0, W, 1024):
+        if k < kv:
+            sign_s(A("UU", k, min(k + 1024, kv)), k, min(k + 1024, kv))
+        if k + 1024 > kv:
+            sign_v(A("UU", max(k, kv), k + 1024), max(k, kv), k + 1024)
+        block(ps(7), "ONE", "X0", k // 256, k // 256 + 4, k == 0, k == W - 1024)
+    climb_rows(CT0)
+    zmake(["B", "A", "C", "IT", "J", "KP", "PO", "PP", "PS", "NN", "BIT", "R1", "R9"])
+    wrap(ps(0, 0, 64), "PAR", "GI1", 0, NI)
+    dma("Y", rows("WT", 0, 0, PA_) + [(A("WT", 0, W, row=14), A("VB"))])
+    dma("Y", [(A("INI", IT_, IT_ + 256), T.itm[:]), (A("BI"), T.bit[:])])
+    dma("Y", rows("D", 0, 0, PA_) + rows("D", 1, 0, NN_) + rows("D", 2, 0, SD_) + rows("D", 3, 0, PA_) + rows("D", 4, 0, NN_))
+    copy(A("OFF0"), ps(0, 0, 64))
+    ts(A("Q0"), ps(0, 0, 64), float(W), op.add)
+
+    def start_extras(s):
+        if s == 1:
+            ts(A("NI4"), A("NI4"), col("RF", 0), op.add)
+            ts(col("THF", 0), col("THI", 0), -1.0, op.mult, 0.5, op.add)
+        if s == 2:
+            split_bits(IT_, IT_ + 256)
+        if s == 3:
+            split_cast(IT_, IT_ + 256)
+            dma("Y", rows("D", 5, 0, IT_))
+        if s == 4:
+            ts(A("FA"), ps(5), 0.0, op.is_equal)
+            tt(A("FA"), A("FA"), A("NI4"), op.mult)
+        if s == 5:
+            tt(A("FA"), ps(5), A("FA"), op.add)
+            copy(A("SCO"), A("FA"))
+            act(A("SIDE"), ps(5))
+        if s == 6:
+            copy(A("BITB"), A("BI"))
+            ts(A("NBIT"), A("BITB"), -1.0, op.mult, 1.0, op.add)
+            copy(A("BROW"), A("BITB"))
+            ts(col("BROW", 0), col("OH", 0), 3.0, op.mult, col("BITB", 0), op.add)
+            dma("Y", [(A("D", row=6), A("BROW")), (A("D", row=7), A("NBIT"))])
+            dma("Y", [(A("UU", W, 2 * W), A("UU", 0, W))])
+        if s == 7:
+            scatter(P["sc_step"])
+
+    for t in range(ROUNDS):
+        last = t == ROUNDS - 1
+        KB, LB_ = "K%d" % t, "LAND%d" % t
+        iv, uv = P["iv"], P["uv"][t]
+        parts = [(a, min(a + 512, NI), 3 + (a - uv) // 512) for a in range(uv, NI, 512)]
+
+        def counts(s):
+            gu = "GU%d" % (s % 2)
+            copy(A("OC", 64 * s, 64 * s + 64), ps(2, 0, 64))
+            o = A("ACC", 0, uv)
+            gi = IX(A("UU", 0, W), A("OC", 64 * s, 64 * s + uv // 16))
+            if s == 0:
+                copy(o, gi)
+            else:
+                tt(o, gi, o, op.add)
+            m = max(uv, NI // 2) if s == STEPS - 1 else uv
+            act(A(gu, m, NI), IX(A("UU", 0, W), A("OC", 64 * s + m // 16, 64 * s + 64)))
+            if m > uv:
+                copy(A(gu, uv, m), IX(A("UU", 0, W), A("OC", 64 * s + uv // 16, 64 * s + m // 16)))
+
+        def counts_add(s):
+            for a, b, bank in parts:
+                mms(ps(bank, 0, b - a), [(A("IDN"), A("GU%d" % (s % 2), a, b))], s == 0, s == STEPS - 1)
+
+        for s in range(STEPS):
+            gi = "GI%d" % (s % 2)
+            on, oo, win = ("OFF0", 0, A("WT", FR, FR + W)) if s == 0 else ("OFF", 64 * s, A("WT"))
+            here = A("Q0") if s == 0 else A("OFFF", 64 * (s % 2), 64 * (s % 2) + 64)
+            nxt = A("OFFF", 64 * ((s + 1) % 2), 64 * ((s + 1) % 2) + 64)
+            copy(A(gi, 0, iv), IX(win, A(on, oo, oo + iv // 16)))
+            act(A(gi, iv, NI), IX(win, A(on, oo + iv // 16, oo + 64)))
+            if s > 0:
+                counts(s - 1)
+            if t == 0:
+                start_extras(s)
+            elif s == 0:
+                copy(A("PARI"), ps(6))
+                tt(A("AB"), A("M"), A("BITB"), op.mult)
+                dma("Y", [(A("D", row=0, rs=8), A("J4", row=0, rs=8)), (A("D", row=3, rs=8), A("J4", row=0, rs=8)),
+                          (A("D", row=7), A("BITB")), (A("D", row=15), A("AB")), (A("TT"), A("UU", 0, W))])
+            if s < STEPS - 1:
+                wrap(ps(0, 0, 64), "B", gi, 0, NI)
+                wrap(ps(1, 0, 64), "A", gi, 0, NI)
+            wrap(ps(2, 0, 64), "C", gi, 0, NI, more=[(A("IDF"), here)])
+            if s > 0:
+                counts_add(s - 1)
+            if t == 0:
+                k = s % 4
+                wrap(ps(5 + s // 4, 64 * k, 64 * k + 64), ("SD", "PAR")[s // 4], "WT", FR + 1024 * k, FR + 1024 * k + 1024)
+            if s < STEPS - 1:
+                tt(A("Q"), ps(0, 0, 64), A("Q0") if s == 0 else A("Q"), op.add)
+                tt(nxt, ps(1, 0, 64), A("Q"), op.min)
+                copy(A("OFF", 64 * s + 64, 64 * s + 128), nxt)
+        counts(STEPS - 1)
+        counts_add(STEPS - 1)
+        for a, b, bank in parts:
+            act(A("ACC", a, b), ps(bank, 0, b - a))
+
+        exchange(lambda r: A("ACC", OWN * r, OWN * r + OWN), A(LB_, OWN * rank, OWN * rank + OWN),
+                 [A(LB_, OWN * T.rank_of(c), OWN * T.rank_of(c) + OWN) for c in peers], "la%d" % t, "l%d" % (2 * t))
+
+        def items_of_parents(a, b):
+            for k in range(a, b, 1024):
+                act(A("PPB", k, k + 1024), IX(A("D"), A("PARI", k // 16, k // 16 + 64)))
+
+        if t == 0:
+            copy(A("PARI"), ps(6))
+            wrap(ps(5), "IT", "D", 0, W)
+            wrap(ps(3), "BIT", "D", 0, W)
+            scatter(P["sc_w"])
+            copy(A("ITI"), ps(5))
+        else:
+            wrap(ps(5), "NN", "INV", 0, W)
+            block(ps(6), "NN", "INV", 0, 16)
+            for k in range(0, W, 1024):
+                tt(A("UU", W + k, W + k + 1024), IX(A("TT"), A("PARI", k // 16, k // 16 + 64)), A("UU", k, k + 1024), op.add)
+            tt(A("NBF"), A("HB", NN_, NN_ + 256), A("LB", NN_, NN_ + 256), op.add)
+            tt(A("FA"), ps(5), A("BV"), op.subtract)
+            tt(A("RBF"), ps(6), A("NBF"), op.subtract)
+            tt(A("FA"), A("FA"), A("SA1"), op.add)
+            tt(A("RBF"), A("RBF"), A("NBIT"), op.mult)
+            copy(A("PT1"), A("FA"))
+        items_of_parents(0, P["pre"][t])
+        srcs = [A("ACC", OWN * rank, OWN * rank + OWN)] + [A(LB_, OWN * T.rank_of(c), OWN * T.rank_of(c) + OWN) for c in peers]
+        mms(ps(0, 0, OWN), [(A("IDN"), x) for x in srcs], True, True)
+        act(A("VI"), ps(0, 0, OWN), fn.Sign, bias=col("THF", 0))
+        mms(ps(1, 0, OWN), [(A("BO"), A("VI"))], True, True)
+        mine = A(KB, OWN * rank, OWN * rank + OWN)
+        act(A("YA", OWN * t, OWN * t + OWN), ps(0, 0, OWN))
+        act(A("VK"), ps(1, 0, OWN), fn.Sign, bias=col("CF", CKB), scale=col("CF", CKS))
+        act(mine, A("VK"), fn.Relu)
+        exchange(lambda r: mine, mine, [A(KB, OWN * T.rank_of(c), OWN * T.rank_of(c) + OWN) for c in peers],
+                 "ka%d" % t, "l%d" % (2 * t + 1))
+        dma("Y", [(T.ya[:, OWN * t:OWN * t + OWN], A("YA", OWN * t, OWN * t + OWN))])
+        items_of_parents(P["pre"][t], W)
+        wrap(ps(4), "IT", "PPB", 0, W)
+        copy(A("IPO"), ps(4))
+        if t == 0:
+            act(A("BIF"), ps(3))
+            for k in range(0, W, 1024):
+                act(A("U1", k, k + 1024), IX(A("UU", 0, W), A("PARI", k // 16, k // 16 + 64)))
+                dma("G", [(A("UU", W + k, W + k + 1024), A("U1", k, k + 1024))], add=True)
+            iota(A("REPF"), [[0, W]], 0, 0)
+
+        for w in range(2):
+            tt(A("X0", H * w, H * w + H), IX(A(KB), A("ITI", 128 * w, 128 * w + 128)), A("D", H * w, H * w + H), op.mult)
+            act(A("KPB", H * w, H * w + H), IX(A(KB), A("IPO", 128 * w, 128 * w + 128)))
+            wrap(ps(w, 0, 128), "J", "X0", H * w, H * w + H)
+            wrap(ps(2, 128 * w, 128 * w + 128), "KP", "KPB", H * w, H * w + H)
+        copy(A("JO0", 0, 128), ps(0, 0, 128))
+        chain = ["X0", "J2", "J4", "J8"]
+        for lv in range(3):
+            src, dst = chain[lv], chain[lv + 1]
+            oi, on = "JO%d" % (lv % 2), "JO%d" % ((lv + 1) % 2)
+            a = P["lv"][t][lv]
+            for w in range(2):
+                c0 = 128 * w
+                vo, vi_ = A(dst, 16 * c0, 16 * (c0 + a)), IX(A(src), A(oi, c0, c0 + a))
+                so, si = A(dst, 16 * (c0 + a), 16 * (c0 + 128)), IX(A(src), A(oi, c0 + a, c0 + 128))
+                if lv == 2:
+                    ts(vo, vi_, col("CF", CJ), op.mult)
+                    act(so, si, fn.Copy, scale=col("CF", CJ))
+                else:
+                    copy(vo, vi_)
+                    act(so, si)
+                if w == 0:
+                    copy(A(oi, 128, 256), ps(1, 0, 128))
+                scatter(W if lv == 1 and w == 1 else P["sc_lv"])
+                if lv < 2:
+                    wrap(ps(w, 0, 128), "J", dst, H * w, H * w + H)
+                if lv == 2 and w == 0:
+                    tt(A("FD"), ps(2), A("NI4"), op.add)
+                    copy(A("PDO"), A("FD"))
+                    if t == 0:
+                        tt(A("SA1"), A("BIF"), A("SIDE"), op.mult)
+                        tt(A("SA0"), A("SIDE"), A("SA1"), op.subtract)
+                if lv == 2 and w == 1 and t == 0:
+                    tt(A("BV"), ps(4), A("BIF"), op.mult)
+                    tt(A("FA"), A("SA0"), A("BV"), op.add)
+                    copy(A("PT0"), A("FA"))
+            if lv < 2:
+                copy(A(on, 0, 128), ps(0, 0, 128))
+            if lv == 1 and t == 0:
+                wrap(ps(4), "NN", "INV", 0, W)
+                block(ps(5, 0, 256), "R1", "INV", 0, 16)
+                block(ps(5, 256, 512), "R9", "INV", 0, 16)
+        gs, pav = P["gs"], P["pav"][t]
+        vch = [1024, 3072] if last else list(range(gs, W, 1024))
+        sch = [k for k in range(0, W, 1024) if k not in vch]
+        for k in vch + sch:
+            act(A("U1", k, k + 1024), IX(A("UU"), A("PDO", k // 16, k // 16 + 64)))
+            if k in vch:
+                dma("Y", [(A("KPB", k, k + 1024), A("U1", k, k + 1024))])
+        XB, XI = 6, (0, 1)
+        for a0, b0 in ((0, H), (H, W - 1024), (W - 1024, W)):
+            tt(A("P1", a0, b0), IX(A("J8"), A("PARI", a0 // 16, b0 // 16)), A("X0", a0, b0), op.add)
+            if a0 == 0:
+                wrap(ps(XI[0], 0, 128), "PS", "P1", 0, H, True, False)
+                wrap(ps(2, 0, 128), "PO", "P1", 0, H)
+            block(ps(XB), "PS", "P1", a0 // 256, b0 // 256, a0 == 0, False)
+        wrap(ps(XI[1], 0, 128), "PS", "P1", H, W, True, False)
+
+        PT, SA = "PT%d" % t, "SA%d" % t
+        a = P["ppv"][t]
+        for w in range(2):
+            c0 = 128 * w
+            copy(A("PPB", 16 * c0, 16 * (c0 + a)), IX(A("P1"), A(PT, c0, c0 + a)))
+            act(A("PPB", 16 * (c0 + a), 16 * (c0 + 128)), IX(A("P1"), A(PT, c0 + a, c0 + 128)))
+            if w == 0:
+                wrap(ps(XI[w], 0, 128), "PP", "PPB", H * w, H * w + H, False, True)
+                block(ps(XB), "PP", "PPB", 0, 8, False, False)
+            else:
+                block(ps(XB), "PP", "PPB", 8, 16, False, True)
+                wrap(ps(XI[w], 0, 128), "PP", "PPB", H * w, H * w + H, False, True)
+        wrap(ps(2, 128, 256), "PO", "P1", H, W)
+        banks = (4, 5, 0, 1)
+
+        def absorb_offsets(w):
+            c0 = 128 * w
+            ts(A("FB", c0, c0 + 128), ps(XI[w], 0, 128), 65536.0, op.is_equal)
+            tt(A("FC", c0, c0 + 128), A("FB", c0, c0 + 128), A(SA, c0, c0 + 128), op.mult)
+            copy(A("GO", c0, c0 + 128), A("FC", c0, c0 + 128))
+
+        def absorb_s(k):
+            act(A("TT", k, k + 1024), IX(A("U1"), A("GO", k // 16, k // 16 + 64)))
+
+        def absorb_v(k):
+            tt(A("TT", k, k + 1024), IX(A("U1"), A("GO", k // 16, k // 16 + 64)), A("KPB", k, k + 1024), op.add)
+
+        def bank_of(k):
+            return ps(banks[2 * sch.index(k // 1024 * 1024) + k % 1024 // 512], 0, 512)
+
+        def add_s(k):
+            for j in (k, k + 512):
+                mms(bank_of(j), [(A("IDN"), A("U1", j, j + 512)), (A("IDN"), A("TT", j, j + 512))], True, True)
+                if not last:
+                    sign_s(bank_of(j), j, j + 512)
+
+        def clip_s(k):
+            for j in (k, k + 512):
+                ts(A("UU", j, j + 512), bank_of(j), 15.0, op.min)
+
+        def clip_v(a0, b0):
+            ts(A("UU", a0, b0), A("TT", a0, b0), 15.0, op.min)
+
+        def counts_out(k):
+            dma("Y", [(T.yc[:, k:k + 1024], A("UU", k, k + 1024))])
+
+        RW, PO_ = ("REPF", "PAO") if last else ("J2", "J4")
+
+        def parents(e, a0, b0):
+            o, i = A(PO_, a0, b0), IX(A(RW), A("P1O", a0 // 16, b0 // 16))
+            if e == "S":
+                act(o, i)
+            else:
+                copy(o, i)
+            q = "S" if e == "S" else "Y"
+            if last:
+                dma(q, [(T.yp[:, a0:b0], A("PAO", a0, b0, row=0))])
+            else:
+                dma(q, [(A("WT", FR + a0, FR + b0, row=0, rs=8), A("J4", a0, b0, row=0, rs=8))])
+
+        absorb_offsets(0)
+        if last:
+            absorb_s(sch[0])
+            absorb_v(vch[0])
+            ts(A("M"), ps(XB), 65536.0, op.is_equal)
+            tt(A("WF"), A("M"), A("RBF"), op.mult)
+            tt(A("WF"), A("WF"), A("NBF"), op.add)
+            dma("Y", [(A("REPF", row=0), A("WF"))])
+            absorb_offsets(1)
+            absorb_s(sch[1])
+            add_s(sch[0])
+            clip_v(vch[0], vch[0] + 1024)
+            counts_out(vch[0])
+            copy(A("P1O"), ps(2))
+            clip_s(sch[0])
+            counts_out(sch[0])
+            absorb_v(vch[1])
+            add_s(sch[1])
+            clip_v(vch[1], vch[1] + 1024)
+            counts_out(vch[1])
+            clip_s(sch[1])
+            counts_out(sch[1])
+        else:
+            for k in sch:
+                absorb_s(k)
+            for hl, src in ((0, "HB"), (256, "LB")):
+                tt(A("RB2", hl, hl + 256), ps(5, hl, hl + 256), A(src, NN_, NN_ + 256), op.subtract)
+            for hl, src in ((0, "HB"), (256, "LB")):
+                tt(A("RB2", hl, hl + 256), A("RB2", hl, hl + 256), A("BITB"), op.mult)
+            ts(A("M"), ps(XB), 65536.0, op.is_equal)
+            for hl, src in ((0, "HB"), (256, "LB")):
+                tt(A("W2", hl, hl + 256), A("M"), A("RB2", hl, hl + 256), op.mult)
+            for hl, src in ((0, "HB"), (256, "LB")):
+                tt(A("W2", hl, hl + 256), A("W2", hl, hl + 256), A(src, NN_, NN_ + 256), op.add)
+                dma("Y", [(A("J2", row=hl // 32), A("W2", hl, hl + 256))])
+            absorb_offsets(1)
+            copy(A("P1O"), ps(2))
+            for k in sch:
+                add_s(k)
+            block(ps(3), "SD", "PPB", 0, 16)
+            block(ps(7), "ONE", "X0", 0, gs // 256, True, False)
+            for k in vch:
+                absorb_v(k)
+                sign_v(A("TT", k, k + 1024), k, k + 1024)
+                block(ps(7), "ONE", "X0", k // 256, k // 256 + 4, False, k == W - 1024)
+            old = A("INI", SD_, SD_ + 256)
+            tt(A("FD"), ps(3), A("NBIT"), op.mult)
+            tt(A("FD"), A("FD"), old, op.subtract)
+            tt(A("FD"), A("FD"), A("M"), op.mult)
+            climb_rows(CT1)
+            tt(old, A("FD"), old, op.add)
+            split(SD_, SD_ + 256)
+            dma("Y", rows("WT", 2, FR, SD_))
+        cuts = [c for c in (0, H, W - 1024, W) if c <= W - pav]
+        for a0, b0 in zip(cuts[:-1], cuts[1:]):
+            parents("S", a0, b0)
+        if pav:
+            parents("V", W - pav, W)
+        if not last:
+            dma("Y", [(A("WT", 0, W, row=0, rs=8), A("J4", row=0, rs=8)), (A("WT", 0, W, row=14), A("VB"))])
+            wrap(ps(6), "PAR", "J4", 0, W)
+            for k in sch[::-1]:
+                clip_s(k)
+            clip_v(gs, W)
+
+    for s in sorted(count):
+        if not any(waited[e].get(s, 0) >= count[s] for e in eng):
+            wait("Y", s, count[s])

@@ -3,48 +3,35 @@ from concourse.mybir import AluOpType, ActivationFunctionType
 
 W, NI, STEPS, ROUNDS = 4096, 1024, 8, 2
 ZW = 144
-ZN = ["A", "B", "C", "PAR", "SD", "IT", "J", "KP", "PO", "PP", "PS", "NN", "BIT", "R1", "R9"]
-PRM = dict(iv=512, uv=(320, 512), kv0=12, gs=2048, pav=(0, 1024), lv=((60, 60, 40), (64, 64, 60)), ppv=(64, 64),
-           sc_step=128, sc_w=3328, sc_lv=128, pre=(4096, 3072))
+ZN = ["HD", "PAR", "C", "SD", "IT", "IB", "K", "U", "EO0", "EO1", "EP0", "EP1", "IV", "PT"]
+PRM = dict(iv=512, uv=(0, 192), gz=2048, sc_a=128, sc_b=128, sc_h0=256, vpre=2048,
+           sum1=(((0, "S"), (1024, "S"), (2048, "S")), ((1024, "S"), (3072, "S"))),
+           sum2=(((3072, "S"),), ((0, "V"), (2048, "V"))),
+           lv=30, ppv=(32, 30, 32, 28), sgv=(1, 2, 3), early=512, pav=(0, 1024), abs_=(1024, 1024))
 
 BF, F32, I32, U16 = "bfloat16", "float32", "int32", "uint16"
-SCRATCH = {
-    "UU": ("sbuf", [128, 2 * W], BF), "U1": ("sbuf", [128, W], BF), "TT": ("sbuf", [128, W], BF),
-    "WT": ("sbuf", [128, 2 * W], BF), "INV": ("sbuf", [128, 2 * W], BF), "D": ("sbuf", [128, W], BF),
-    "X0": ("sbuf", [128, W], BF), "J2": ("sbuf", [128, W], BF), "J4": ("sbuf", [128, W], BF),
-    "J8": ("sbuf", [128, W], BF), "P1": ("sbuf", [128, W], BF), "PPB": ("sbuf", [128, W], BF),
-    "KPB": ("sbuf", [128, W], BF),
-    "REPF": ("sbuf", [128, W], F32), "PAO": ("sbuf", [128, W], F32),
-    "GI0": ("sbuf", [128, NI], BF), "GI1": ("sbuf", [128, NI], BF),
-    "GU0": ("sbuf", [128, NI], BF), "GU1": ("sbuf", [128, NI], BF),
-    "ACC": ("sbuf", [128, NI], BF), "K0": ("sbuf", [128, NI], BF), "K1": ("sbuf", [128, NI], BF),
-    "LAND0": ("sbuf", [128, NI], BF), "LAND1": ("sbuf", [128, NI], BF),
-    "VI": ("sbuf", [128, 256], BF), "VK": ("sbuf", [128, 256], BF), "YA": ("sbuf", [128, 512], F32),
-    "INI": ("sbuf", [128, 1088], I32), "HI": ("sbuf", [128, 576], I32), "LO": ("sbuf", [128, 576], I32),
-    "HB": ("sbuf", [128, 1088], BF), "LB": ("sbuf", [128, 1088], BF),
-    "BI": ("sbuf", [128, 256], I32), "BITB": ("sbuf", [128, 256], BF), "NBIT": ("sbuf", [128, 256], BF),
-    "BROW": ("sbuf", [128, 256], BF), "RB2": ("sbuf", [128, 512], BF), "M": ("sbuf", [128, 256], BF),
-    "W2": ("sbuf", [128, 512], BF), "AB": ("sbuf", [128, 256], BF), "VB": ("sbuf", [128, 256], BF),
-    "NBF": ("sbuf", [128, 256], F32), "RBF": ("sbuf", [128, 256], F32), "WF": ("sbuf", [128, 256], F32),
-    "NI4": ("sbuf", [128, 256], F32), "FA": ("sbuf", [128, 256], F32), "FB": ("sbuf", [128, 256], F32),
-    "FC": ("sbuf", [128, 256], F32), "FD": ("sbuf", [128, 256], F32), "SIDE": ("sbuf", [128, 256], F32),
-    "SA0": ("sbuf", [128, 256], F32), "SA1": ("sbuf", [128, 256], F32), "BIF": ("sbuf", [128, 256], F32),
-    "BV": ("sbuf", [128, 256], F32),
-    "SCO": ("sbuf", [128, 256], U16), "PARI": ("sbuf", [128, 256], U16), "ITI": ("sbuf", [128, 256], U16),
-    "IPO": ("sbuf", [128, 256], U16), "PDO": ("sbuf", [128, 256], U16), "JO0": ("sbuf", [128, 256], U16),
-    "JO1": ("sbuf", [128, 256], U16), "PT0": ("sbuf", [128, 256], U16), "PT1": ("sbuf", [128, 256], U16),
-    "GO": ("sbuf", [128, 256], U16), "P1O": ("sbuf", [128, 256], U16),
-    "OFF0": ("sbuf", [128, 64], U16), "OFF": ("sbuf", [128, 512], U16), "OC": ("sbuf", [128, 512], U16),
-    "Q0": ("sbuf", [128, 64], F32), "Q": ("sbuf", [128, 64], F32), "OFFF": ("sbuf", [128, 128], F32),
-    "ZS": ("sbuf", [128, ZW * len(ZN)], BF), "Z1": ("sbuf", [128, ZW], BF), "ONE": ("sbuf", [128, 128], BF),
-    "BO": ("sbuf", [128, 128], BF), "IDN": ("sbuf", [128, 128], BF), "IDF": ("sbuf", [128, 128], F32),
-    "RI": ("sbuf", [128, 8], I32), "RJ": ("sbuf", [128, 8], I32), "RF": ("sbuf", [128, 8], F32),
-    "IO16": ("sbuf", [128, 16], F32), "OH": ("sbuf", [128, 16], F32), "OP": ("sbuf", [128, 8], F32),
-    "CF": ("sbuf", [128, 16], F32), "THI": ("sbuf", [128, 4], I32), "THF": ("sbuf", [128, 4], F32),
-}
+SCRATCH = {}
+for _n, _w in (("UU", 2 * W + 16), ("U1", W), ("TT", 2 * W + 16), ("WT", 2 * W), ("INV", 2 * W), ("PPB", W), ("X0", W), ("J2", W),
+               ("J4", W), ("KN", W), ("P1", W), ("PP", W), ("GI0", NI), ("GI1", NI), ("GU0", NI), ("GU1", NI),
+               ("ACC", NI), ("K0", NI + 32), ("K1", NI + 32), ("LAND0", NI), ("LAND1", NI), ("VI", 256),
+               ("HB", 1088), ("LB", 1088), ("BITB", 256), ("BROW", 256), ("SB2", 512), ("RB2", 512), ("M", 256),
+               ("MW", 256), ("W2", 512), ("AB", 256), ("VB", 256), ("NHI", 256), ("ZS", ZW * len(ZN)), ("Z1", ZW),
+               ("ONE", 128), ("BO", 128), ("IDN", 128), ("NID", 128), ("RT", 128), ("SEL", 96), ("Z0", 128)):
+    SCRATCH[_n] = ("sbuf", [128, _w], BF)
+for _n, _w in (("REPF", W), ("PAO", W), ("YA", 512), ("NW", 256), ("NI4", 256), ("RBF", 256), ("WF", 256), ("FA", 256),
+               ("FD", 256), ("SA0", 256), ("SA1", 256), ("BIF", 256), ("NBF", 256), ("BV", 256),
+               ("NV", 256), ("XI", 256), ("SIDE", 256), ("Q", 128), ("NX", 136), ("IDF", 128), ("RF32", 128), ("RF", 8),
+               ("IO16", 16), ("OH", 16), ("OP", 8), ("PN", 8), ("PU", 8), ("CF", 32), ("THF", 4)):
+    SCRATCH[_n] = ("sbuf", [128, _w], F32)
+for _n, _w in (("INI", 1088), ("HI", 256), ("LO", 256), ("IVI", 256), ("BI", 256), ("RI", 8), ("RJ", 8), ("THI", 4)):
+    SCRATCH[_n] = ("sbuf", [128, _w], I32)
+for _n, _w in (("SCO", 256), ("PARI", 256), ("ITI0", 256), ("ITI1", 256), ("IPO", 256), ("UL", 256), ("JO0", 256),
+               ("JO1", 256), ("JO2", 256), ("PT0", 256), ("PT1", 256), ("GO", 256), ("P1O", 256), ("OFF0", 64),
+               ("OFF", 512), ("OC", 512)):
+    SCRATCH[_n] = ("sbuf", [128, _w], U16)
 for _b in range(8):
     SCRATCH["ps%d" % _b] = ("psum", [128, 512], F32)
-NDS = 70
+NDS = 80
 SEMAPHORES = ["cV", "cS", "cP", "cG", "la0", "la1", "ka0", "ka1", "l0", "l1", "l2", "l3"] + ["d%d" % _i for _i in range(NDS)]
 ESZ = {BF: 2, F32: 4, I32: 4, U16: 2}
 
@@ -161,14 +148,19 @@ def rank_program(g, core, T, topo):
     def asel(o, i, pat, cmp, base, cm):
         comp("G", lambda: g.affine_select(o[0], i[0], pat, cmp, 0.0, base, cm), [o], [i])
 
-    def mms(o, terms, start, stop):
-        ins = [x for t in terms for x in t]
-        sync("P", "P", regs(ins), regs([o]))
+    def mmx(items):
+        ins = [x for it in items for x in it[1:3]]
+        outs = [it[0] for it in items]
+        sync("P", "P", regs(ins), regs(outs))
         count["cP"] = count.get("cP", 0) + 1
-        for k, (l, r) in enumerate(terms):
-            h = g.tensor.matmul(o[0], l[0], r[0], start and k == 0, stop and k == len(terms) - 1)
+        for o, l, r, st, sp in items:
+            h = g.tensor.matmul(o[0], l[0], r[0], st, sp)
         h.then_inc(T.sem["cP"], 1)
-        note("P", ("cP", count["cP"]), regs(ins), regs([o]))
+        note("P", ("cP", count["cP"]), regs(ins), regs(outs))
+
+    def mms(o, terms, start, stop):
+        n = len(terms)
+        mmx([(o, l, r, start and k == 0, stop and k == n - 1) for k, (l, r) in enumerate(terms)])
 
     def Z(z, i):
         if z == "ONE":
@@ -221,29 +213,30 @@ def rank_program(g, core, T, topo):
     def col(name, j):
         return A(name, j, j + 1)
 
-    def ps(b, a=0, e=256):
-        return A("ps%d" % b, a, e)
+    def ps(b, a=0, e=256, step=1):
+        return A("ps%d" % b, a, e, step)
 
     FR = W
     H = W // 2
     NN_, PA_, SD_, HD_, IT_ = 0, 256, 512, 768, 832
-    CA, CB, CC, CJ, CD, CPO, CPE, CPP, CPS, CKP, CKS, CKB, CT0, CT1, CX = range(15)
+    (CA, CB, CC, CK, CG, CIB, CEO, CEP, CPT, CX, CNAT, CTAU, CKA, CKB, CM1, C15, C120, C1, CPE,
+     CO1, CP0, CP1, CDP, CGK, CT) = range(25)
+    ES = 262144.0
 
-    def rows(dst, r, a, src_off, n=256, wd=W):
+    def rows(dst, r, a, src_off, wd=W, n=256):
         return [(A(dst, a, a + wd, row=r), A("HB", src_off, src_off + n)),
                 (A(dst, a, a + wd, row=r + 8), A("LB", src_off, src_off + n))]
 
-    def split_bits(a, b):
-        ts(A("HI", 0, b - a), A("INI", a, b), 4032, op.bitwise_and)
-        ts(A("LO", 0, b - a), A("INI", a, b), 63, op.bitwise_and)
+    def split_bits(a):
+        ts(A("HI"), A("INI", a, a + 256), 4, op.logical_shift_right)
+        ts(A("LO"), A("INI", a, a + 256), 15, op.bitwise_and)
+        copy(A("HB", a, a + 256), A("HI"))
+        copy(A("LB", a, a + 256), A("LO"))
 
-    def split_cast(a, b):
-        copy(A("HB", a, b), A("HI", 0, b - a))
-        copy(A("LB", a, b), A("LO", 0, b - a))
-
-    def split(a, b):
-        split_bits(a, b)
-        split_cast(a, b)
+    def split_round(a, n, src=None):
+        src = src or A("INI", a, a + n)
+        copy(A("HB", a, a + n), src)
+        tt(A("LB", a, a + n), src, A("HB", a, a + n), op.subtract)
 
     sc_done = [0]
 
@@ -252,24 +245,21 @@ def rank_program(g, core, T, topo):
         n = min(n, W - a)
         if n > 0:
             off = A("SCO", a // 16, (a + n) // 16)
-            src = A("WT", FR + a, FR + a + n)
+            src = A("WT", a, a + n)
             comp("V", lambda: g.vector.tensor_copy(IX(A("INV"), off)[0], src[0]), [A("INV")], [src], off[1])
             sc_done[0] = a + n
 
     def sign_v(src, a, b):
-        ts(A("X0", a, b), src, 3.5, op.is_ge)
+        ts(A("X0", a, b), src, 3.5, op.is_ge, 0.5, op.subtract)
 
     def sign_s(src, a, b):
         act(A("X0", a, b), src, fn.Sign, bias=col("CF", CX))
-
-    def climb_rows(ct):
-        ts(A("VB"), ps(7), col("CF", ct), op.subtract, 1.0, op.is_lt)
-        dma("Y", [(A("WT", FR, FR + W, row=14), A("VB"))])
 
     dma("Y", [(A("INI", PA_, PA_ + 256), T.par[:]), (A("INI", SD_, SD_ + 256), T.side[:]),
               (A("INI", HD_, HD_ + 64), T.heads[:])])
     for k in range(4):
         dma("Y", [(A("UU", 1024 * k, 1024 * k + 1024), T.cnt[:, 1024 * k:1024 * k + 1024])])
+    gz = P["gz"]
     iota(A("INI", NN_, NN_ + 256), [[1, 256]], 0, 256, False)
     iota(col("RI", 0), [[0, 1]], 0, 1, False)
     iota(A("IO16"), [[1, 16]], 0, 0)
@@ -277,306 +267,410 @@ def rank_program(g, core, T, topo):
     iota(A("Z1"), [[0, ZW]], 0, 0)
     asel(A("Z1", 15, 128, 16), A("ONE", 0, 8), [[-16, 8]], op.is_ge, 0, 1)
     asel(A("Z1", 15, 128, 16), A("Z1", 15, 128, 16), [[16, 8]], op.is_ge, 15, -1)
+    iota(A("SEL", 0, 64), [[0, 64]], 0, 0)
+    for h in range(2):
+        asel(A("RT", 64 * h, 64 * h + 64), A("ONE", 0, 64), [[-2, 64]], op.is_equal, -h, 1)
     asel(A("IDN"), A("ONE"), [[-1, 128]], op.is_equal, 0, 1)
-    iota(A("WT", 0, W), [[0, W]], 0, 0)
     iota(A("NI4"), [[16, 256]], W, 0)
-    dma("G", [(col("THI", 0), T.th[:])], slow=True)
-    iota(A("D"), [[0, W]], 0, 0)
+    iota(A("WT", 0, gz), [[0, gz]], 0, 0)
     iota(A("INV", 0, W), [[0, W]], 0, 0)
+    dma("G", [(col("THI", 0), T.th[:])], slow=True)
     asel(A("BO"), A("ONE"), [[-16, 8], [0, 16]], op.is_ge, 0, 1)
     asel(A("BO"), A("BO"), [[16, 8], [0, 16]], op.is_ge, 15, -1)
+    iota(A("NHI"), [[1, 256]], 0, 0)
+    iota(A("Z0"), [[0, 128]], 0, 0)
+    iota(A("REPF"), [[0, W]], 0, 0)
 
     memset(A("WT", FR, FR + W), 1.0)
-    memset(col("CF", CX), -3.5)
+    for c, v in ((CX, -3.5), (CM1, -1.0), (C1, 1.0)):
+        memset(col("CF", c), v)
+    ts(A("INI", NN_, NN_ + 256), A("INI", NN_, NN_ + 256), W - 1, op.bitwise_and)
+    split_bits(NN_)
+    dma("S", rows("WT", 1, FR, NN_) + rows("WT", 3, FR, NN_))
+    memset(A("GI1"), 0.0)
+    split_bits(PA_)
+    split_round(SD_, 320)
+    dma("Y", rows("GI1", 0, 0, HD_, NI, 64))
+    dma("Y", rows("WT", 2, FR, SD_) + rows("WT", 0, FR, PA_))
+    if gz < W:
+        memset(A("WT", gz, W), 0.0)
     ts(col("RJ", 0), col("RI", 0), 15, op.bitwise_and)
     ts(col("RJ", 1), col("RI", 0), 7, op.bitwise_and)
-    split(NN_, NN_ + 256)
-    dma("S", rows("WT", 1, FR, NN_))
     copy(A("RF", 0, 2), A("RJ", 0, 2))
-    memset(A("GI1"), 0.0)
     ts(A("OH"), A("IO16"), col("RF", 0), op.is_equal)
     ts(A("OP"), A("IO16", 0, 8), col("RF", 1), op.is_equal)
-    split(PA_, IT_)
-    dma("Y", rows("GI1", 0, 0, HD_, 64, NI))
-    dma("Y", rows("WT", 2, FR, SD_) + rows("WT", 0, FR, PA_))
-    ts(col("CF", CT0), col("RF", 0), float(P["kv0"]), op.is_ge, 7.5, op.mult)
-    ts(col("CF", CA), col("OH", 14), 8192.0, op.mult, col("OP", 0), op.add)
-    ts(col("CF", CB), col("OP", 2), col("OP", 1), op.subtract)
-    ts(col("CF", CC), col("OH", 14), 2.0, op.mult, col("OH", 15), op.add)
-    ts(col("CF", CJ), col("OP", 0), col("OP", 1), op.add)
-    ts(col("CF", CD), col("OP", 3), col("OP", 4), op.add)
-    ts(col("CF", CPE), col("OH", 6), 8.0, op.mult, col("OP", 7), op.add)
-    ts(col("CF", CKP), col("OH", 1), -4096.0, op.mult)
-    ts(col("CF", CKS), col("OP", 1), col("OP", 4), op.add)
-    ts(col("CF", CKB), col("OP", 2), col("OH", 6), op.add, col("OH", 15), op.add)
-    ts(col("CF", CT1), col("RF", 0), float(P["gs"] // 256), op.is_ge, 7.5, op.mult)
-    ts(col("CF", CC), col("CF", CC), -4096.0, op.mult)
-    ts(col("CF", CPO), col("CF", CJ), col("CF", CD), op.subtract)
-    ts(col("CF", CKS), col("CF", CKS), 2.0, op.mult, -1.0, op.add)
-    ts(col("CF", CPP), col("CF", CPE), 8192.0, op.mult, col("CF", CPO), op.add)
-    ts(col("CF", CPS), col("CF", CPE), 8192.0, op.mult, col("CF", CPO), op.subtract)
-    ts(col("CF", CKB), col("CF", CKB), 100.0, op.mult, col("CF", CKS), op.subtract)
-    zcol = {"A": col("CF", CA), "B": col("CF", CB), "C": col("CF", CC), "PAR": col("OP", 0),
-            "SD": col("OP", 2), "IT": col("OP", 5), "J": col("CF", CJ), "KP": col("CF", CKP), "PO": col("CF", CPO),
-            "PP": col("CF", CPP), "PS": col("CF", CPS), "NN": col("OP", 1), "BIT": col("OH", 6),
-            "R1": col("OH", 1), "R9": col("OH", 9)}
+    ts(col("CF", CNAT), col("RF", 0), 8.0, op.is_lt, 15.0, op.mult)
+    ts(col("CF", CTAU), col("RF", 0), 8.0, op.is_ge, 255.0, op.mult)
+    ts(A("CF", CNAT, CTAU + 1), A("CF", CNAT, CTAU + 1), 1.0, op.add)
+    ts(A("PN"), A("OP"), col("CF", CNAT), op.mult)
+    ts(A("PU"), A("OP"), col("CF", CTAU), op.mult)
+    ts(col("CF", CA), col("OH", 14), 8192.0, op.mult, col("PN", 0), op.add)
+    ts(col("CF", CB), col("OP", 2), col("PN", 1), op.subtract)
+    ts(col("CF", CC), col("OH", 14), -8192.0, op.mult, col("PN", 3), op.add)
+    memset(A("NX", 0, 8), 0.0)
+
+    def late_consts():
+        ts(col("CF", CK), col("PN", 1), col("PN", 2), op.add)
+        ts(col("CF", CIB), col("OH", 6), 1024.0, op.mult, col("OP", 5), op.add)
+        ts(col("CF", CPT), col("PU", 0), col("PU", 3), op.add)
+        ts(col("CF", CPE), col("OH", 6), 0.25, op.mult, col("OH", 7), op.add)
+        ts(col("CF", CKA), col("OP", 2), col("OP", 3), op.add, col("OP", 0), op.subtract)
+        ts(col("CF", CPE), col("CF", CPE), 0.125, op.mult)
+        ts(col("CF", CKA), col("CF", CKA), col("OP", 1), op.subtract, col("OH", 7), op.subtract)
+        ts(col("CF", CEO), col("CF", CPE), col("CF", CPT), op.add, ES, op.mult)
+        ts(col("CF", CEP), col("CF", CPE), col("CF", CPT), op.subtract, ES, op.mult)
+        ts(col("CF", CKA), col("CF", CKA), col("OH", 14), op.subtract, col("OH", 15), op.subtract)
+        ts(col("CF", CDP), col("OH", 15), 4096.0, op.mult)
+        ts(col("CF", CT), col("OH", 15), 0.5, op.mult, col("OH", 14), op.add)
+        ts(col("CF", CO1), col("OH", 13), ES / 8, op.mult, col("CF", CEO), op.add)
+        ts(col("CF", CP1), col("OH", 13), ES / 8, op.mult, col("CF", CEP), op.add)
+        ts(col("CF", CP0), col("CF", CT), 4096.0, op.mult, col("CF", CEP), op.add)
+        ts(col("CF", CT), col("OH", 15), 0.5, op.mult, col("OH", 14), op.subtract)
+        ts(col("CF", CGK), col("OP", 0), col("OP", 1), op.add, col("OP", 2), op.add)
+        ts(col("CF", CKB), col("CF", CKA), 8.5, op.mult)
+        ts(col("CF", CP1), col("CF", CT), 4096.0, op.mult, col("CF", CP1), op.add)
+        ts(col("CF", CGK), col("CF", CGK), col("OP", 3), op.add)
+        ts(col("CF", CG), col("OP", 5), -1.0, op.mult)
+        for c, v in ((C15, 15.0), (C120, 120.0)):
+            memset(col("CF", c), v)
+        for kb in ("K0", "K1"):
+            memset(A(kb, 0, 16), 0.0)
+            memset(A(kb, NI + 16, NI + 32), 0.0)
+        memset(A("UU", 2 * W, 2 * W + 16), 0.0)
+        memset(A("TT", 2 * W, 2 * W + 16), 0.0)
+
+    zcol = {"HD": col("OP", 0), "PAR": col("PN", 0), "C": col("CF", CC), "SD": col("OP", 2), "IT": col("OP", 5),
+            "IB": col("CF", CIB), "K": col("CF", CK), "U": col("CF", CDP), "EO0": col("CF", CEO), "EO1": col("CF", CO1),
+            "EP0": col("CF", CP0), "EP1": col("CF", CP1), "IV": col("PU", 3), "PT": col("CF", CPT)}
 
     def zmake(names):
         for z in names:
             o = ZN.index(z) * ZW
             act(A("ZS", o, o + ZW), A("Z1"), fn.Copy, scale=zcol[z])
 
-    kv = 256 * P["kv0"]
-    zmake(["PAR", "SD"])
-    act(A("IDF"), A("IDN"))
     for k in range(0, W, 1024):
-        if k < kv:
-            sign_s(A("UU", k, min(k + 1024, kv)), k, min(k + 1024, kv))
-        if k + 1024 > kv:
-            sign_v(A("UU", max(k, kv), k + 1024), max(k, kv), k + 1024)
+        sign_s(A("UU", k, k + 1024), k, k + 1024)
         block(ps(7), "ONE", "X0", k // 256, k // 256 + 4, k == 0, k == W - 1024)
-    climb_rows(CT0)
-    zmake(["B", "A", "C", "IT", "J", "KP", "PO", "PP", "PS", "NN", "BIT", "R1", "R9"])
-    wrap(ps(0, 0, 64), "PAR", "GI1", 0, NI)
-    dma("Y", rows("WT", 0, 0, PA_) + [(A("WT", 0, W, row=14), A("VB"))])
+    act(A("VB"), ps(7), fn.Relu, bias=col("CF", C1), scale=col("CF", CM1))
+    dma("S", [(A("WT", FR, FR + W, row=14), A("VB"))])
+    zmake(["HD"])
+    wrap(ps(1, 0, 64), "HD", "GI1", 0, NI)
+    for j, c in ((0, col("OP", 2)), (16, col("CF", CA)), (32, col("CF", CB)), (48, col("CF", CA))):
+        act(A("SEL", j, j + 16, 2), A("Z1", 15, 128, 16), fn.Copy, scale=c)
+    act(A("RF32"), A("RT"))
+    zmake(["C", "PAR", "SD"])
+    act(A("IDF"), A("IDN"))
+    act(A("NID"), A("IDN"), fn.Copy, scale=col("CF", CM1))
+    dma("Y", rows("WT", 0, 0, PA_) + rows("WT", 3, 0, NN_) + [(A("WT", 0, W, row=14), A("VB"))])
     dma("Y", [(A("INI", IT_, IT_ + 256), T.itm[:]), (A("BI"), T.bit[:])])
-    dma("Y", rows("D", 0, 0, PA_) + rows("D", 1, 0, NN_) + rows("D", 2, 0, SD_) + rows("D", 3, 0, PA_) + rows("D", 4, 0, NN_))
-    copy(A("OFF0"), ps(0, 0, 64))
-    ts(A("Q0"), ps(0, 0, 64), float(W), op.add)
+    late_consts()
+    ts(A("NI4"), A("NI4"), col("RF", 0), op.add)
+    ts(A("FA"), A("INI", SD_, SD_ + 256), 0.0, op.is_equal)
+    tt(A("FA"), A("FA"), A("NI4"), op.mult)
+    tt(A("FA"), A("FA"), A("INI", SD_, SD_ + 256), op.add)
+    copy(A("OFF0"), ps(1, 0, 64))
+    copy(A("SCO"), A("FA"))
+    zmake(["IT", "IB", "K", "U", "EO0", "EO1", "EP0", "EP1", "IV", "PT"])
+    for j, c in ((64, col("CF", CEO)), (72, col("CF", CG)), (80, col("CF", CEP)), (88, col("OP", 4))):
+        act(A("SEL", j, j + 8), A("Z1", 15, 128, 16), fn.Copy, scale=c)
 
-    def start_extras(s):
-        if s == 1:
-            ts(A("NI4"), A("NI4"), col("RF", 0), op.add)
-            ts(col("THF", 0), col("THI", 0), -1.0, op.mult, 0.5, op.add)
-        if s == 2:
-            split_bits(IT_, IT_ + 256)
-        if s == 3:
-            split_cast(IT_, IT_ + 256)
-            dma("Y", rows("D", 5, 0, IT_))
-        if s == 4:
-            ts(A("FA"), ps(5), 0.0, op.is_equal)
-            tt(A("FA"), A("FA"), A("NI4"), op.mult)
-        if s == 5:
-            tt(A("FA"), ps(5), A("FA"), op.add)
-            copy(A("SCO"), A("FA"))
-            act(A("SIDE"), ps(5))
-        if s == 6:
-            copy(A("BITB"), A("BI"))
-            ts(A("NBIT"), A("BITB"), -1.0, op.mult, 1.0, op.add)
-            copy(A("BROW"), A("BITB"))
-            ts(col("BROW", 0), col("OH", 0), 3.0, op.mult, col("BITB", 0), op.add)
-            dma("Y", [(A("D", row=6), A("BROW")), (A("D", row=7), A("NBIT"))])
-            dma("Y", [(A("UU", W, 2 * W), A("UU", 0, W))])
-        if s == 7:
-            scatter(P["sc_step"])
+    def extras_a(t, s):
+        if t == 0:
+            if s == 1:
+                copy(A("HB", IT_, IT_ + 256), A("INI", IT_, IT_ + 256))
+            if s == 2:
+                copy(A("BITB"), A("BI"))
+            if s == 3:
+                ts(A("BROW"), A("BITB"), -0.5, op.add)
+                ts(col("BROW", 0), col("OH", 0), 4.0, op.mult, col("BROW", 0), op.add)
+            if s == 4:
+                tt(A("SB2", 0, 256), A("HB", SD_, SD_ + 256), A("BITB"), op.mult)
+            if s == 5:
+                tt(A("SB2", 256, 512), A("LB", SD_, SD_ + 256), A("BITB"), op.mult)
+            if s == 6:
+                ts(A("NW"), A("NI4"), float(W), op.subtract)
+                copy(col("THF", 0), col("THI", 0))
+            if s >= 2:
+                scatter(P["sc_a"])
+        else:
+            if s == 2:
+                ts(A("ITI1"), A("XI"), -496.0, op.add, 1040.0, op.min)
+
+    def extras_b(t, s):
+        if t == 0:
+            if s == 1:
+                tt(A("LB", IT_, IT_ + 256), A("INI", IT_, IT_ + 256), A("HB", IT_, IT_ + 256), op.subtract)
+            elif 2 <= s < STEPS - 1:
+                scatter(P["sc_b"])
+        else:
+            if s == 0:
+                copy(A("PARI"), ps(6))
+            if s == 1:
+                tt(A("SA1"), A("SIDE"), A("SA0"), op.subtract)
+            if s == 2:
+                tt(A("RBF"), A("NV"), A("NW"), op.subtract)
+            if s == 3:
+                tt(A("NV"), A("NV"), A("BV"), op.subtract)
+            if s == 4:
+                tt(A("FA"), A("SA1"), A("NV"), op.add)
+            if s == 5:
+                copy(A("PT1"), A("FA"))
 
     for t in range(ROUNDS):
         last = t == ROUNDS - 1
         KB, LB_ = "K%d" % t, "LAND%d" % t
+        US, UD = ("UU", "TT") if t == 0 else ("TT", "UU")
         iv, uv = P["iv"], P["uv"][t]
-        parts = [(a, min(a + 512, NI), 3 + (a - uv) // 512) for a in range(uv, NI, 512)]
+        parts = [(uv, 512, 3), (512, NI, 4)] + ([(0, uv, 5)] if last and uv else [])
 
         def counts(s):
             gu = "GU%d" % (s % 2)
             copy(A("OC", 64 * s, 64 * s + 64), ps(2, 0, 64))
-            o = A("ACC", 0, uv)
-            gi = IX(A("UU", 0, W), A("OC", 64 * s, 64 * s + uv // 16))
-            if s == 0:
-                copy(o, gi)
+            m = 512 if s == STEPS - 1 else uv
+
+            def ix(a, b):
+                return IX(A(US, 0, W), A("OC", 64 * s + a // 16, 64 * s + b // 16))
+            if last:
+                if m:
+                    ts(A(gu, 0, m), ix(0, m), 15.0, op.min)
+                act(A(gu, m, NI), ix(m, NI), fn.Relu, bias=col("CF", C15), scale=col("CF", CM1))
             else:
-                tt(o, gi, o, op.add)
-            m = max(uv, NI // 2) if s == STEPS - 1 else uv
-            act(A(gu, m, NI), IX(A("UU", 0, W), A("OC", 64 * s + m // 16, 64 * s + 64)))
-            if m > uv:
-                copy(A(gu, uv, m), IX(A("UU", 0, W), A("OC", 64 * s + uv // 16, 64 * s + m // 16)))
+                if uv and s == 0:
+                    copy(A("ACC", 0, uv), ix(0, uv))
+                elif uv:
+                    tt(A("ACC", 0, uv), ix(0, uv), A("ACC", 0, uv), op.add)
+                act(A(gu, m, NI), ix(m, NI))
+                if m > uv:
+                    copy(A(gu, uv, m), ix(uv, m))
 
         def counts_add(s):
             for a, b, bank in parts:
-                mms(ps(bank, 0, b - a), [(A("IDN"), A("GU%d" % (s % 2), a, b))], s == 0, s == STEPS - 1)
+                neg = last and (a >= 512 or (a >= uv and s < STEPS - 1))
+                mms(ps(bank, 0, b - a), [(A("NID" if neg else "IDN"), A("GU%d" % (s % 2), a, b))], s == 0, s == STEPS - 1)
 
         for s in range(STEPS):
             gi = "GI%d" % (s % 2)
             on, oo, win = ("OFF0", 0, A("WT", FR, FR + W)) if s == 0 else ("OFF", 64 * s, A("WT"))
-            here = A("Q0") if s == 0 else A("OFFF", 64 * (s % 2), 64 * (s % 2) + 64)
-            nxt = A("OFFF", 64 * ((s + 1) % 2), 64 * ((s + 1) % 2) + 64)
             copy(A(gi, 0, iv), IX(win, A(on, oo, oo + iv // 16)))
             act(A(gi, iv, NI), IX(win, A(on, oo + iv // 16, oo + 64)))
+            if s == STEPS - 1 and t == 0:
+                dma("Y", rows("WT", 5, FR, IT_) + [(A("WT", FR, FR + W, row=6), A("BROW"))])
             if s > 0:
                 counts(s - 1)
-            if t == 0:
-                start_extras(s)
-            elif s == 0:
-                copy(A("PARI"), ps(6))
-                tt(A("AB"), A("M"), A("BITB"), op.mult)
-                dma("Y", [(A("D", row=0, rs=8), A("J4", row=0, rs=8)), (A("D", row=3, rs=8), A("J4", row=0, rs=8)),
-                          (A("D", row=7), A("BITB")), (A("D", row=15), A("AB")), (A("TT"), A("UU", 0, W))])
+            extras_a(t, s)
             if s < STEPS - 1:
-                wrap(ps(0, 0, 64), "B", gi, 0, NI)
-                wrap(ps(1, 0, 64), "A", gi, 0, NI)
-            wrap(ps(2, 0, 64), "C", gi, 0, NI, more=[(A("IDF"), here)])
+                so = 0 if s == 0 else 32
+                mmx([(ps(0, ch, 256, 8), A(gi, ch, NI, 8), A("SEL", so, so + 32), True, True) for ch in range(8)])
+                if s == 0:
+                    ts(A("Q"), ps(0, 0, 128), float(W), op.add)
+                else:
+                    tt(A("Q"), ps(0, 0, 128), A("Q"), op.add)
+                tt(A("NX", 8, 136), ps(0, 128, 256), A("Q"), op.min)
+                mms(ps(1, 0, 64), [(A("NX", 8, 136), A("RF32", 0, 64)), (A("NX", 0, 128), A("RF32", 64, 128))], True, True)
+            wrap(ps(2, 0, 64), "C", gi, 0, NI)
             if s > 0:
                 counts_add(s - 1)
-            if t == 0:
-                k = s % 4
-                wrap(ps(5 + s // 4, 64 * k, 64 * k + 64), ("SD", "PAR")[s // 4], "WT", FR + 1024 * k, FR + 1024 * k + 1024)
+            extras_b(t, s)
             if s < STEPS - 1:
-                tt(A("Q"), ps(0, 0, 64), A("Q0") if s == 0 else A("Q"), op.add)
-                tt(nxt, ps(1, 0, 64), A("Q"), op.min)
-                copy(A("OFF", 64 * s + 64, 64 * s + 128), nxt)
+                copy(A("OFF", 64 * s + 64, 64 * s + 128), ps(1, 0, 64))
         counts(STEPS - 1)
         counts_add(STEPS - 1)
         for a, b, bank in parts:
-            act(A("ACC", a, b), ps(bank, 0, b - a))
+            o, i = A("ACC", a, b), ps(bank, 0, b - a)
+            if a >= 512:
+                if last:
+                    act(o, i, fn.Identity, bias=col("CF", C120))
+                else:
+                    act(o, i)
+            elif last and a >= uv:
+                ts(o, i, 105.0, op.add)
+            else:
+                copy(o, i)
 
         exchange(lambda r: A("ACC", OWN * r, OWN * r + OWN), A(LB_, OWN * rank, OWN * rank + OWN),
                  [A(LB_, OWN * T.rank_of(c), OWN * T.rank_of(c) + OWN) for c in peers], "la%d" % t, "l%d" % (2 * t))
+        vpre = P["vpre"] if last else 0
 
-        def items_of_parents(a, b):
-            for k in range(a, b, 1024):
-                act(A("PPB", k, k + 1024), IX(A("D"), A("PARI", k // 16, k // 16 + 64)))
+        def above(k):
+            o, i = A("PPB", k, k + 1024), IX(A("WT", FR, FR + W), A("PARI", k // 16, k // 16 + 64))
+            if k < vpre:
+                copy(o, i)
+            else:
+                act(o, i)
+
+        def above_list(k):
+            wrap(ps(2 + k // H, k % H // 16, k % H // 16 + 64), "IT", "PPB", k, k + 1024)
+            dma("Y", [(A("PPB", k, k + 1024, row=2, rs=8), A("WT", FR + k, FR + k + 1024, row=1, rs=8)),
+                      (A("PPB", k, k + 1024, row=14), A("WT", FR + k, FR + k + 1024, row=6))])
+
+        def summed(k, e):
+            o, i = A(US, W + k, W + k + 1024), IX(A(US, 0, W), A("PARI", k // 16, k // 16 + 64))
+            if e == "V":
+                copy(o, i)
+            else:
+                act(o, i)
+
+        def summed_add(k):
+            dma("G", [(A(US, W + k, W + k + 1024), A(US, k, k + 1024))], add=True)
 
         if t == 0:
-            copy(A("PARI"), ps(6))
-            wrap(ps(5), "IT", "D", 0, W)
-            wrap(ps(3), "BIT", "D", 0, W)
-            scatter(P["sc_w"])
-            copy(A("ITI"), ps(5))
-        else:
-            wrap(ps(5), "NN", "INV", 0, W)
-            block(ps(6), "NN", "INV", 0, 16)
             for k in range(0, W, 1024):
-                tt(A("UU", W + k, W + k + 1024), IX(A("TT"), A("PARI", k // 16, k // 16 + 64)), A("UU", k, k + 1024), op.add)
-            tt(A("NBF"), A("HB", NN_, NN_ + 256), A("LB", NN_, NN_ + 256), op.add)
-            tt(A("FA"), ps(5), A("BV"), op.subtract)
-            tt(A("RBF"), ps(6), A("NBF"), op.subtract)
-            tt(A("FA"), A("FA"), A("SA1"), op.add)
-            tt(A("RBF"), A("RBF"), A("NBIT"), op.mult)
-            copy(A("PT1"), A("FA"))
-        items_of_parents(0, P["pre"][t])
+                wrap(ps(5 + k // 1024 % 2, 0, 64), "PAR", "WT", k, k + 1024)
+                copy(A("PARI", k // 16, k // 16 + 64), ps(5 + k // 1024 % 2, 0, 64))
+                above(k)
+                scatter(P["sc_h0"])
+            wrap(ps(7), "IB", "WT", FR, FR + W)
+            scatter(W)
+        else:
+            for k in range(0, W, 1024):
+                above(k)
+        for k, e in P["sum1"][t]:
+            summed(k, e)
+        above_list(0)
+        above_list(1024)
+        if t == 0:
+            wrap(ps(5), "SD", "WT", FR, FR + W)
         srcs = [A("ACC", OWN * rank, OWN * rank + OWN)] + [A(LB_, OWN * T.rank_of(c), OWN * T.rank_of(c) + OWN) for c in peers]
         mms(ps(0, 0, OWN), [(A("IDN"), x) for x in srcs], True, True)
-        act(A("VI"), ps(0, 0, OWN), fn.Sign, bias=col("THF", 0))
+        ts(A("VI"), ps(0, 0, OWN), col("THF", 0), op.is_ge)
         mms(ps(1, 0, OWN), [(A("BO"), A("VI"))], True, True)
-        mine = A(KB, OWN * rank, OWN * rank + OWN)
-        act(A("YA", OWN * t, OWN * t + OWN), ps(0, 0, OWN))
-        act(A("VK"), ps(1, 0, OWN), fn.Sign, bias=col("CF", CKB), scale=col("CF", CKS))
-        act(mine, A("VK"), fn.Relu)
-        exchange(lambda r: mine, mine, [A(KB, OWN * T.rank_of(c), OWN * T.rank_of(c) + OWN) for c in peers],
+        mine = A(KB, 16 + OWN * rank, 16 + OWN * rank + OWN)
+        ts(mine, ps(1, 0, OWN), col("CF", CKA), op.mult, col("CF", CKB), op.is_gt)
+        exchange(lambda r: mine, mine, [A(KB, 16 + OWN * T.rank_of(c), 16 + OWN * T.rank_of(c) + OWN) for c in peers],
                  "ka%d" % t, "l%d" % (2 * t + 1))
-        dma("Y", [(T.ya[:, OWN * t:OWN * t + OWN], A("YA", OWN * t, OWN * t + OWN))])
-        items_of_parents(P["pre"][t], W)
-        wrap(ps(4), "IT", "PPB", 0, W)
-        copy(A("IPO"), ps(4))
         if t == 0:
-            act(A("BIF"), ps(3))
-            for k in range(0, W, 1024):
-                act(A("U1", k, k + 1024), IX(A("UU", 0, W), A("PARI", k // 16, k // 16 + 64)))
-                dma("G", [(A("UU", W + k, W + k + 1024), A("U1", k, k + 1024))], add=True)
-            iota(A("REPF"), [[0, W]], 0, 0)
+            wrap(ps(4), "IV", "INV", 0, W)
+        above_list(2048)
+        above_list(3072)
+        act(A("YA", OWN * t, OWN * t + OWN), ps(0, 0, OWN))
+        dma("Y", [(T.ya[:, OWN * t:OWN * t + OWN], A("YA", OWN * t, OWN * t + OWN))])
+        ts(A("IPO", 0, 128), ps(2, 0, 128), 16.0, op.add)
+        for k, e in P["sum2"][t]:
+            summed(k, e)
+        for k in range(0, W, 1024):
+            summed_add(k)
+        if t == 0:
+            ts(A("ITI0"), ps(7), 528.0, op.add, 1040.0, op.min)
+            ts(A("BIF"), ps(7), 512.0, op.is_ge)
+            ts(A("NBF"), ps(7), 512.0, op.is_lt)
+            act(A("XI"), ps(7))
+            tt(A("SA0"), ps(5), A("NBF"), op.mult)
+            act(A("SIDE"), ps(5))
+            tt(A("BV"), ps(4), A("BIF"), op.mult)
+            copy(A("IVI"), ps(4))
+            act(A("NV"), ps(4))
+            tt(A("FA"), A("SA0"), A("BV"), op.add)
+            copy(A("PT0"), A("FA"))
+            ts(A("HI"), A("IVI"), 4, op.logical_shift_right)
+            ts(A("LO"), A("IVI"), 15, op.bitwise_and)
+            tt(A("RB2", 0, 256), A("HI"), A("NHI"), op.subtract)
+            ts(A("RB2", 256, 512), A("LO"), col("RF", 0), op.subtract)
+        ts(A("IPO", 128, 256), ps(3, 0, 128), 16.0, op.add)
 
-        for w in range(2):
-            tt(A("X0", H * w, H * w + H), IX(A(KB), A("ITI", 128 * w, 128 * w + 128)), A("D", H * w, H * w + H), op.mult)
-            act(A("KPB", H * w, H * w + H), IX(A(KB), A("IPO", 128 * w, 128 * w + 128)))
-            wrap(ps(w, 0, 128), "J", "X0", H * w, H * w + H)
-            wrap(ps(2, 128 * w, 128 * w + 128), "KP", "KPB", H * w, H * w + H)
-        copy(A("JO0", 0, 128), ps(0, 0, 128))
-        chain = ["X0", "J2", "J4", "J8"]
-        for lv in range(3):
+        Q4 = range(4)
+
+        def qs(q):
+            return 1024 * q, 1024 * q + 1024
+
+        def take(name, q):
+            copy(A(name, 64 * q, 64 * q + 64), ps(q, 0, 64))
+
+        for q in Q4:
+            a0, b0 = qs(q)
+            tt(A("X0", a0, b0), IX(A(KB), A("IPO", 64 * q, 64 * q + 64)), A("PPB", a0, b0), op.mult)
+            if q:
+                take("JO0", q - 1)
+            wrap(ps(q, 0, 64), "K", "X0", a0, b0)
+            if q % 2:
+                a0 -= 1024
+                act(A("KN", a0, b0), IX(A(KB), A("ITI%d" % t, a0 // 16, b0 // 16)), fn.Copy, scale=col("OH", 7))
+                st = [(A("KN", a0, b0, row=6), A("WT", FR + a0, FR + b0, row=6)),
+                      (A("KN", a0, b0, row=14), A("X0", a0, b0, row=14)), (A("KN", a0, b0, row=15), A("X0", a0, b0, row=15))]
+                if not last:
+                    st.append((A("KN", a0, b0, row=5, rs=8), A("WT", FR + a0, FR + b0, row=2, rs=8)))
+                dma("Y", st)
+            if q == 1:
+                wrap(ps(4, 0, 128), "U", "X0", 0, H, more=[(A("IDF"), A("NW", 0, 128))])
+        if last:
+            dma("Y", [(A("KN", row=13), A("AB"))])
+        else:
+            dma("Y", [(A("KN", row=4), A("SB2", 0, 256)), (A("KN", row=12), A("SB2", 256, 512))])
+        chain = ["X0", "J2", "J4"]
+        for lv in range(2):
             src, dst = chain[lv], chain[lv + 1]
-            oi, on = "JO%d" % (lv % 2), "JO%d" % ((lv + 1) % 2)
-            a = P["lv"][t][lv]
-            for w in range(2):
-                c0 = 128 * w
+            oi, on = "JO%d" % lv, "JO%d" % (lv + 1)
+            a = P["lv"]
+            for q in Q4:
+                c0 = 64 * q
                 vo, vi_ = A(dst, 16 * c0, 16 * (c0 + a)), IX(A(src), A(oi, c0, c0 + a))
-                so, si = A(dst, 16 * (c0 + a), 16 * (c0 + 128)), IX(A(src), A(oi, c0 + a, c0 + 128))
-                if lv == 2:
-                    ts(vo, vi_, col("CF", CJ), op.mult)
-                    act(so, si, fn.Copy, scale=col("CF", CJ))
+                so, si = A(dst, 16 * (c0 + a), 16 * (c0 + 64)), IX(A(src), A(oi, c0 + a, c0 + 64))
+                if lv:
+                    ts(vo, vi_, col("CF", CGK), op.mult)
+                    act(so, si, fn.Copy, scale=col("CF", CGK))
                 else:
                     copy(vo, vi_)
                     act(so, si)
-                if w == 0:
-                    copy(A(oi, 128, 256), ps(1, 0, 128))
-                scatter(W if lv == 1 and w == 1 else P["sc_lv"])
-                if lv < 2:
-                    wrap(ps(w, 0, 128), "J", dst, H * w, H * w + H)
-                if lv == 2 and w == 0:
-                    tt(A("FD"), ps(2), A("NI4"), op.add)
-                    copy(A("PDO"), A("FD"))
-                    if t == 0:
-                        tt(A("SA1"), A("BIF"), A("SIDE"), op.mult)
-                        tt(A("SA0"), A("SIDE"), A("SA1"), op.subtract)
-                if lv == 2 and w == 1 and t == 0:
-                    tt(A("BV"), ps(4), A("BIF"), op.mult)
-                    tt(A("FA"), A("SA0"), A("BV"), op.add)
-                    copy(A("PT0"), A("FA"))
-            if lv < 2:
-                copy(A(on, 0, 128), ps(0, 0, 128))
-            if lv == 1 and t == 0:
-                wrap(ps(4), "NN", "INV", 0, W)
-                block(ps(5, 0, 256), "R1", "INV", 0, 16)
-                block(ps(5, 256, 512), "R9", "INV", 0, 16)
-        gs, pav = P["gs"], P["pav"][t]
-        vch = [1024, 3072] if last else list(range(gs, W, 1024))
-        sch = [k for k in range(0, W, 1024) if k not in vch]
-        for k in vch + sch:
-            act(A("U1", k, k + 1024), IX(A("UU"), A("PDO", k // 16, k // 16 + 64)))
-            if k in vch:
-                dma("Y", [(A("KPB", k, k + 1024), A("U1", k, k + 1024))])
-        XB, XI = 6, (0, 1)
-        for a0, b0 in ((0, H), (H, W - 1024), (W - 1024, W)):
-            tt(A("P1", a0, b0), IX(A("J8"), A("PARI", a0 // 16, b0 // 16)), A("X0", a0, b0), op.add)
-            if a0 == 0:
-                wrap(ps(XI[0], 0, 128), "PS", "P1", 0, H, True, False)
-                wrap(ps(2, 0, 128), "PO", "P1", 0, H)
-            block(ps(XB), "PS", "P1", a0 // 256, b0 // 256, a0 == 0, False)
-        wrap(ps(XI[1], 0, 128), "PS", "P1", H, W, True, False)
+                if q == 0 and lv == 0:
+                    take(oi, 3)
+                elif q == 1 and lv == 0:
+                    copy(A("UL", 0, 128), ps(4, 0, 128))
+                elif q < 2:
+                    take(oi, q + 2)
+                if q >= 2:
+                    take(on, q - 2)
+                wrap(ps(q, 0, 64), "K", dst, 1024 * q, 1024 * q + 1024)
+        wrap(ps(4, 128, 256), "U", "X0", H, W, more=[(A("IDF"), A("NW", 128, 256))])
 
-        PT, SA = "PT%d" % t, "SA%d" % t
-        a = P["ppv"][t]
-        for w in range(2):
-            c0 = 128 * w
-            copy(A("PPB", 16 * c0, 16 * (c0 + a)), IX(A("P1"), A(PT, c0, c0 + a)))
-            act(A("PPB", 16 * (c0 + a), 16 * (c0 + 128)), IX(A("P1"), A(PT, c0 + a, c0 + 128)))
-            if w == 0:
-                wrap(ps(XI[w], 0, 128), "PP", "PPB", H * w, H * w + H, False, True)
-                block(ps(XB), "PP", "PPB", 0, 8, False, False)
-            else:
-                block(ps(XB), "PP", "PPB", 8, 16, False, True)
-                wrap(ps(XI[w], 0, 128), "PP", "PPB", H * w, H * w + H, False, True)
-        wrap(ps(2, 128, 256), "PO", "P1", H, W)
-        banks = (4, 5, 0, 1)
+        def dropped(a0, b0):
+            act(A("U1", a0, b0), IX(A(US), A("UL", a0 // 16, b0 // 16)))
 
-        def absorb_offsets(w):
-            c0 = 128 * w
-            ts(A("FB", c0, c0 + 128), ps(XI[w], 0, 128), 65536.0, op.is_equal)
-            tt(A("FC", c0, c0 + 128), A("FB", c0, c0 + 128), A(SA, c0, c0 + 128), op.mult)
-            copy(A("GO", c0, c0 + 128), A("FC", c0, c0 + 128))
+        dropped(0, H)
+        XB = 5
+        SA, PT = "SA%d" % t, "PT%d" % t
 
-        def absorb_s(k):
-            act(A("TT", k, k + 1024), IX(A("U1"), A("GO", k // 16, k // 16 + 64)))
+        def own_list(w):
+            wrap(ps(w, 0, 128), "PT", "P1", H * w, H * w + H)
 
-        def absorb_v(k):
-            tt(A("TT", k, k + 1024), IX(A("U1"), A("GO", k // 16, k // 16 + 64)), A("KPB", k, k + 1024), op.add)
+        def own_take(w):
+            copy(A("P1O", 128 * w, 128 * w + 128), ps(w, 0, 128))
 
-        def bank_of(k):
-            return ps(banks[2 * sch.index(k // 1024 * 1024) + k % 1024 // 512], 0, 512)
+        def turned(src, so, c0, c1, stop=False):
+            mmx([(ps(XB, 256 * (ch % 2) + ch // 2, 256 * (ch % 2) + 256, 16), A(src, 128 * ch, 128 * ch + 128),
+                  A("SEL", so, so + 16), False, stop and ch == c1 - 1) for ch in range(c0, c1)])
 
-        def add_s(k):
-            for j in (k, k + 512):
-                mms(bank_of(j), [(A("IDN"), A("U1", j, j + 512)), (A("IDN"), A("TT", j, j + 512))], True, True)
-                if not last:
-                    sign_s(bank_of(j), j, j + 512)
+        if not last:
+            mms(ps(XB, 0, 512), [(A("Z0"), A("X0", 0, 512))], True, False)
+        for q in Q4:
+            a0, b0 = qs(q)
+            tt(A("P1", a0, b0), IX(A("J4"), A("JO2", a0 // 16, b0 // 16)), A("KN", a0, b0), op.add)
+            if q < 2:
+                take("JO2", q + 2)
+            if q == 1:
+                copy(A("UL", 128, 256), ps(4, 128, 256))
+                dropped(H, W)
+            wrap(ps(q, 0, 64), "EO%d" % t, "P1", a0, b0, True, False)
+            if not last and q < 3:
+                turned("P1", 64, 8 * q, 8 * q + 8)
 
-        def clip_s(k):
-            for j in (k, k + 512):
-                ts(A("UU", j, j + 512), bank_of(j), 15.0, op.min)
+        def decide(q):
+            c0 = 64 * q
+            ts(A("GO", c0, c0 + 64), ps(q, 0, 64), float(2 * W), op.min)
+            ts(A("MW", c0, c0 + 64), ps(q, 0, 64), 0.0, op.is_equal)
 
-        def clip_v(a0, b0):
-            ts(A("UU", a0, b0), A("TT", a0, b0), 15.0, op.min)
+        a = P["ppv"]
+        for q in Q4:
+            c0 = 64 * q
+            copy(A("PP", 16 * c0, 16 * (c0 + a[q])), IX(A("P1"), A(PT, c0, c0 + a[q])))
+            act(A("PP", 16 * (c0 + a[q]), 16 * (c0 + 64)), IX(A("P1"), A(PT, c0 + a[q], c0 + 64)))
+            if q >= 2:
+                decide(q - 2)
+            wrap(ps(q, 0, 64), "EP%d" % t, "PP", 1024 * q, 1024 * q + 1024, False, True, more=[(A("IDF"), A(SA, c0, c0 + 64))])
 
-        def counts_out(k):
-            dma("Y", [(T.yc[:, k:k + 1024], A("UU", k, k + 1024))])
+        def absorb_v(a0, b0):
+            tt(A(UD, a0, b0), IX(A(US), A("GO", a0 // 16, b0 // 16)), A("U1", a0, b0), op.add)
+
+        def counts_out(a0, b0):
+            dma("Y", [(T.yc[:, a0:b0], A("UU", a0, b0))])
 
         RW, PO_ = ("REPF", "PAO") if last else ("J2", "J4")
 
@@ -586,76 +680,88 @@ def rank_program(g, core, T, topo):
                 act(o, i)
             else:
                 copy(o, i)
-            q = "S" if e == "S" else "Y"
             if last:
-                dma(q, [(T.yp[:, a0:b0], A("PAO", a0, b0, row=0))])
+                dma("Y", [(T.yp[:, a0:b0], A("PAO", a0, b0, row=0))])
             else:
-                dma(q, [(A("WT", FR + a0, FR + b0, row=0, rs=8), A("J4", a0, b0, row=0, rs=8))])
+                dma("Y", [(A("WT", FR + a0, FR + b0, row=0, rs=8), A("J4", a0, b0, row=0, rs=8))])
 
-        absorb_offsets(0)
+        pav, sa = P["pav"][t], P["abs_"][t]
         if last:
-            absorb_s(sch[0])
-            absorb_v(vch[0])
-            ts(A("M"), ps(XB), 65536.0, op.is_equal)
-            tt(A("WF"), A("M"), A("RBF"), op.mult)
-            tt(A("WF"), A("WF"), A("NBF"), op.add)
+            for j in range(0, sa, 512):
+                act(A("GI0", j, j + 512), IX(A(US), A("GO", j // 16, j // 16 + 32)))
+            decide(2)
+            if P["early"]:
+                absorb_v(sa, sa + P["early"])
+            decide(3)
+            tt(A("WF"), A("MW"), A("RBF"), op.mult)
+            tt(A("WF"), A("WF"), A("NW"), op.add)
             dma("Y", [(A("REPF", row=0), A("WF"))])
-            absorb_offsets(1)
-            absorb_s(sch[1])
-            add_s(sch[0])
-            clip_v(vch[0], vch[0] + 1024)
-            counts_out(vch[0])
-            copy(A("P1O"), ps(2))
-            clip_s(sch[0])
-            counts_out(sch[0])
-            absorb_v(vch[1])
-            add_s(sch[1])
-            clip_v(vch[1], vch[1] + 1024)
-            counts_out(vch[1])
-            clip_s(sch[1])
-            counts_out(sch[1])
+            own_list(0)
+            for j in range(0, sa, 512):
+                mms(ps(4 + j // 512, 0, 512), [(A("IDN"), A("U1", j, j + 512)), (A("IDN"), A("GI0", j, j + 512))], True, True)
+            own_list(1)
+            for a0 in range(sa, W, 1024):
+                b0 = min(a0 + 1024, W)
+                if a0 == sa + 1024:
+                    own_take(1)
+                absorb_v(a0 + (P["early"] if a0 == sa else 0), b0)
+                ts(A("UU", a0, b0), A("UU", a0, b0), 15.0, op.min)
+                counts_out(a0, b0)
+                if a0 == sa:
+                    own_take(0)
+                    for j in range(0, sa, 512):
+                        ts(A("UU", j, j + 512), ps(4 + j // 512, 0, 512), 15.0, op.min)
+                    if sa:
+                        counts_out(0, sa)
         else:
-            for k in sch:
-                absorb_s(k)
-            for hl, src in ((0, "HB"), (256, "LB")):
-                tt(A("RB2", hl, hl + 256), ps(5, hl, hl + 256), A(src, NN_, NN_ + 256), op.subtract)
-            for hl, src in ((0, "HB"), (256, "LB")):
-                tt(A("RB2", hl, hl + 256), A("RB2", hl, hl + 256), A("BITB"), op.mult)
-            ts(A("M"), ps(XB), 65536.0, op.is_equal)
-            for hl, src in ((0, "HB"), (256, "LB")):
-                tt(A("W2", hl, hl + 256), A("M"), A("RB2", hl, hl + 256), op.mult)
-            for hl, src in ((0, "HB"), (256, "LB")):
-                tt(A("W2", hl, hl + 256), A("W2", hl, hl + 256), A(src, NN_, NN_ + 256), op.add)
-                dma("Y", [(A("J2", row=hl // 32), A("W2", hl, hl + 256))])
-            absorb_offsets(1)
-            copy(A("P1O"), ps(2))
-            for k in sch:
-                add_s(k)
-            block(ps(3), "SD", "PPB", 0, 16)
-            block(ps(7), "ONE", "X0", 0, gs // 256, True, False)
-            for k in vch:
-                absorb_v(k)
-                sign_v(A("TT", k, k + 1024), k, k + 1024)
-                block(ps(7), "ONE", "X0", k // 256, k // 256 + 4, False, k == W - 1024)
-            old = A("INI", SD_, SD_ + 256)
-            tt(A("FD"), ps(3), A("NBIT"), op.mult)
-            tt(A("FD"), A("FD"), old, op.subtract)
-            tt(A("FD"), A("FD"), A("M"), op.mult)
-            climb_rows(CT1)
-            tt(old, A("FD"), old, op.add)
-            split(SD_, SD_ + 256)
-            dma("Y", rows("WT", 2, FR, SD_))
-        cuts = [c for c in (0, H, W - 1024, W) if c <= W - pav]
+            for j in range(0, sa, 1024):
+                act(A("TT", j, j + 1024), IX(A(US), A("GO", j // 16, j // 16 + 64)))
+                dma("G", [(A("TT", j, j + 1024), A("U1", j, j + 1024))], add=True)
+            decide(2)
+            if P["early"]:
+                absorb_v(sa, sa + P["early"])
+            decide(3)
+            tt(A("W2", 0, 256), A("MW"), A("RB2", 0, 256), op.mult)
+            tt(A("W2", 256, 512), A("MW"), A("RB2", 256, 512), op.mult)
+            tt(A("W2", 0, 256), A("W2", 0, 256), A("NHI"), op.add)
+            ts(A("W2", 256, 512), A("W2", 256, 512), col("RF", 0), op.add)
+            dma("Y", [(A("J2", row=0), A("W2", 0, 256)), (A("J2", row=8), A("W2", 256, 512))])
+            turned("P1", 64, 24, 32)
+            turned("PP", 80, 0, 32, True)
+            own_list(0)
+            order = list(range(sa, W, 1024)) + list(range(0, sa, 1024))
+            for n, k in enumerate(order):
+                if k >= sa:
+                    absorb_v(k + (P["early"] if k == sa else 0), k + 1024)
+                if n == 0:
+                    for h in range(2):
+                        ts(A("M", 128 * h, 128 * h + 128), ps(XB, 256 * h, 256 * h + 128), 0.0, op.is_equal)
+                        tt(A("FD", 128 * h, 128 * h + 128), ps(XB, 256 * h + 128, 256 * h + 256), A("M", 128 * h, 128 * h + 128), op.mult)
+                    mmx([(ps(4), A("IDN"), A("HB", SD_, SD_ + 256), True, False), (ps(4), A("IDN"), A("LB", SD_, SD_ + 256), False, False),
+                         (ps(4, 0, 128), A("FD", 0, 128), A("IDF"), False, False), (ps(4, 128, 256), A("FD", 128, 256), A("IDF"), False, True)])
+                    mmx([(ps(6, 128 * h, 128 * h + 128), A("M", 128 * h, 128 * h + 128), A("IDN"), True, True) for h in range(2)])
+                    own_list(1)
+                    own_take(0)
+                if n == 1:
+                    split_round(SD_, 256, ps(4))
+                    dma("Y", rows("WT", 2, FR, SD_))
+                    own_take(1)
+                if n in P["sgv"]:
+                    sign_v(A("TT", k, k + 1024), k, k + 1024)
+                else:
+                    sign_s(A("TT", k, k + 1024), k, k + 1024)
+                block(ps(7), "ONE", "X0", k // 256, k // 256 + 4, n == 0, n == 3)
+        cuts = [c for c in (0, 1024, H, W - 1024, W) if c <= W - pav]
         for a0, b0 in zip(cuts[:-1], cuts[1:]):
             parents("S", a0, b0)
-        if pav:
-            parents("V", W - pav, W)
+        for a0 in range(W - pav, W, 1024):
+            parents("V", a0, min(a0 + 1024, W))
         if not last:
-            dma("Y", [(A("WT", 0, W, row=0, rs=8), A("J4", row=0, rs=8)), (A("WT", 0, W, row=14), A("VB"))])
+            ts(A("VB"), ps(7), 0.25, op.is_lt)
+            dma("S", [(A("WT", FR, FR + W, row=14), A("VB"))])
+            tt(A("AB"), ps(6), A("BITB"), op.mult)
             wrap(ps(6), "PAR", "J4", 0, W)
-            for k in sch[::-1]:
-                clip_s(k)
-            clip_v(gs, W)
+            dma("Y", [(A("WT", 0, W, row=0, rs=8), A("J4", row=0, rs=8)), (A("WT", 0, W, row=14), A("VB"))])
 
     for s in sorted(count):
         if not any(waited[e].get(s, 0) >= count[s] for e in eng):

from concourse.bass import DstId, RemoteDMATransfer
from concourse.mybir import AluOpType, ActivationFunctionType

W, NI, STEPS, ROUNDS = 4096, 1024, 8, 2
ZW = 144
ZN = ["HD", "PAR", "C", "SD", "IT", "IB", "K", "U", "EO0", "EO1", "EP0", "EP1", "IV", "PT"]
PRM = dict(iv=512, uv=(0, 192), gz=2048, sc_a=128, sc_b=128, sc_h0=256, vpre=2048,
           sum1=(((0, "S"), (1024, "S"), (2048, "S")), ((1024, "S"), (3072, "S"))),
           sum2=(((3072, "S"),), ((0, "V"), (2048, "V"))),
           lv=30, ppv=(32, 30, 32, 28), sgv=(1, 2, 3), early=512, pav=(0, 1024), abs_=(1024, 1024))

BF, F32, I32, U16 = "bfloat16", "float32", "int32", "uint16"
SCRATCH = {}
for _n, _w in (("UU", 2 * W + 16), ("U1", W), ("TT", 2 * W + 16), ("WT", 2 * W), ("INV", 2 * W), ("PPB", W), ("X0", W), ("J2", W),
               ("J4", W), ("KN", W), ("P1", W), ("PP", W), ("GI0", NI), ("GI1", NI), ("GU0", NI), ("GU1", NI),
               ("ACC", NI), ("K0", NI + 32), ("K1", NI + 32), ("LAND0", NI), ("LAND1", NI), ("VI", 256),
               ("HB", 1088), ("LB", 1088), ("BITB", 256), ("BROW", 256), ("SB2", 512), ("RB2", 512), ("M", 256),
               ("MW", 256), ("W2", 512), ("AB", 256), ("VB", 256), ("NHI", 256), ("ZS", ZW * len(ZN)), ("Z1", ZW),
               ("ONE", 128), ("BO", 128), ("IDN", 128), ("NID", 128), ("RT", 128), ("SEL", 96), ("Z0", 128)):
    SCRATCH[_n] = ("sbuf", [128, _w], BF)
for _n, _w in (("REPF", W), ("PAO", W), ("YA", 512), ("NW", 256), ("NI4", 256), ("RBF", 256), ("WF", 256), ("FA", 256),
               ("FD", 256), ("SA0", 256), ("SA1", 256), ("BIF", 256), ("NBF", 256), ("BV", 256),
               ("NV", 256), ("XI", 256), ("SIDE", 256), ("Q", 128), ("NX", 136), ("IDF", 128), ("RF32", 128), ("RF", 8),
               ("IO16", 16), ("OH", 16), ("OP", 8), ("PN", 8), ("PU", 8), ("CF", 32), ("THF", 4)):
    SCRATCH[_n] = ("sbuf", [128, _w], F32)
for _n, _w in (("INI", 1088), ("HI", 256), ("LO", 256), ("IVI", 256), ("BI", 256), ("RI", 8), ("RJ", 8), ("THI", 4)):
    SCRATCH[_n] = ("sbuf", [128, _w], I32)
for _n, _w in (("SCO", 256), ("PARI", 256), ("ITI0", 256), ("ITI1", 256), ("IPO", 256), ("UL", 256), ("JO0", 256),
               ("JO1", 256), ("JO2", 256), ("PT0", 256), ("PT1", 256), ("GO", 256), ("P1O", 256), ("OFF0", 64),
               ("OFF", 512), ("OC", 512)):
    SCRATCH[_n] = ("sbuf", [128, _w], U16)
for _b in range(8):
    SCRATCH["ps%d" % _b] = ("psum", [128, 512], F32)
NDS = 80
SEMAPHORES = ["cV", "cS", "cP", "cG", "la0", "la1", "ka0", "ka1", "l0", "l1", "l2", "l3"] + ["d%d" % _i for _i in range(NDS)]
ESZ = {BF: 2, F32: 4, I32: 4, U16: 2}


def rank_program(g, core, T, topo):
    rank = T.rank_of(core)
    if rank is None:
        return
    P = PRM
    NR = len(T.cores)
    OWN = NI // NR
    op = AluOpType
    fn = ActivationFunctionType
    eng = {"V": g.vector, "S": g.scalar, "P": g.tensor, "G": g, "Y": g.sync}
    count = {}
    waited = {e: {} for e in eng}
    hist = {}
    nds = [0]

    def A(name, a=None, b=None, step=1, row=None, rs=16):
        wd = SCRATCH[name][1][1]
        a = 0 if a is None else a
        b = wd if b is None else b
        es = ESZ[SCRATCH[name][2]]
        if SCRATCH[name][0] == "psum":
            reg = (name, 0xFFFF, 0, 2048)
        else:
            m = 0xFFFF if row is None else sum(1 << r for r in range(row, 16, rs))
            reg = (name, m, a * es, b * es)
        ps = slice(None) if row is None else slice(row, None, rs)
        cs = slice(a, b) if step == 1 else slice(a, b, step)
        return (T[name][ps, cs], [reg])

    def IX(win, off):
        return (win[0].indirect(off[0]), win[1] + off[1])

    def wait(e, sem, val):
        if waited[e].get(sem, 0) < val:
            eng[e].wait_ge(T.sem[sem], val)
            waited[e][sem] = val

    def sync(e, who, reads, writes):
        need = {}
        for rg, wr in ((reads, False), (writes, True)):
            for (nm, m, lo, hi) in rg:
                psum = nm.startswith("ps")
                for (m2, lo2, hi2, who2, tok, wr2) in hist.get(nm, []):
                    if not (m & m2) or hi <= lo2 or hi2 <= lo:
                        continue
                    if psum:
                        hit = who != who2
                    else:
                        hit = wr or wr2
                    if hit:
                        need[tok[0]] = max(need.get(tok[0], 0), tok[1])
        for s in sorted(need):
            wait(e, s, need[s])

    def note(who, tok, reads, writes):
        for rg, wr in ((reads, False), (writes, True)):
            for (nm, m, lo, hi) in rg:
                h = hist.setdefault(nm, [])
                if wr or nm.startswith("ps"):
                    h[:] = [x for x in h if not ((x[0] & ~m) == 0 and lo <= x[1] and x[2] <= hi)]
                else:
                    h[:] = [x for x in h if not (who is not None and x[3] == who and not x[5]
                                                 and (x[0] & ~m) == 0 and lo <= x[1] and x[2] <= hi)]
                h.append((m, lo, hi, who, tok, wr))

    def regs(xs):
        return [r for x in xs if isinstance(x, tuple) for r in x[1]]

    def raw(x):
        return x[0] if isinstance(x, tuple) else x

    def comp(e, call, outs, ins, offs=()):
        sync(e, e, regs(ins) + list(offs), regs(outs))
        s = "c" + e
        count[s] = count.get(s, 0) + 1
        call().then_inc(T.sem[s], 1)
        note(e, (s, count[s]), regs(ins) + list(offs), regs(outs))

    def copy(o, i):
        comp("V", lambda: g.vector.tensor_copy(o[0], i[0]), [o], [i])

    def tt(o, a, b, f):
        comp("V", lambda: g.vector.tensor_tensor(o[0], a[0], b[0], f), [o], [a, b])

    def ts(o, a, s1, f0, s2=None, f1=None):
        if f1 is None:
            comp("V", lambda: g.vector.tensor_scalar(o[0], a[0], raw(s1), None, f0), [o], [a, s1])
        else:
            comp("V", lambda: g.vector.tensor_scalar(o[0], a[0], raw(s1), raw(s2), f0, f1), [o], [a, s1, s2])

    def memset(o, v):
        comp("V", lambda: g.vector.memset(o[0], v), [o], [])

    def act(o, i, f=fn.Copy, bias=None, scale=None):
        if bias is not None and scale is not None:
            comp("S", lambda: g.scalar.activation(o[0], i[0], f, bias=raw(bias), scale=raw(scale)), [o], [i, bias, scale])
        elif bias is not None:
            comp("S", lambda: g.scalar.activation(o[0], i[0], f, bias=raw(bias)), [o], [i, bias])
        elif scale is not None:
            comp("S", lambda: g.scalar.activation(o[0], i[0], f, scale=raw(scale)), [o], [i, scale])
        else:
            comp("S", lambda: g.scalar.activation(o[0], i[0], f), [o], [i])

    def iota(o, pat, base, cm, flt=True):
        if flt:
            comp("G", lambda: g.iota(o[0], pat, base, cm, allow_small_or_imprecise_dtypes=True), [o], [])
        else:
            comp("G", lambda: g.iota(o[0], pat, base, cm), [o], [])

    def asel(o, i, pat, cmp, base, cm):
        comp("G", lambda: g.affine_select(o[0], i[0], pat, cmp, 0.0, base, cm), [o], [i])

    def mmx(items):
        ins = [x for it in items for x in it[1:3]]
        outs = [it[0] for it in items]
        sync("P", "P", regs(ins), regs(outs))
        count["cP"] = count.get("cP", 0) + 1
        for o, l, r, st, sp in items:
            h = g.tensor.matmul(o[0], l[0], r[0], st, sp)
        h.then_inc(T.sem["cP"], 1)
        note("P", ("cP", count["cP"]), regs(ins), regs(outs))

    def mms(o, terms, start, stop):
        n = len(terms)
        mmx([(o, l, r, start and k == 0, stop and k == n - 1) for k, (l, r) in enumerate(terms)])

    def Z(z, i):
        if z == "ONE":
            return A("Z1", 15 - i, 143 - i)
        o = ZN.index(z) * ZW
        return A("ZS", o + 15 - i, o + 143 - i)

    def wrap(o, z, src, a, b, start=True, stop=True, more=()):
        mms(o, [(Z(z, i), A(src, a + i, b, 16)) for i in range(16)] + list(more), start, stop)

    def block(o, z, src, q0, q1, start=True, stop=True):
        mms(o, [(Z(z, i), A(src, 256 * i, 256 * i + 256)) for i in range(q0, q1)], start, stop)

    def dma(e, pairs, add=False, slow=False):
        s = "d%d" % nds[0]
        nds[0] += 1
        sync(e, None, regs([p[1] for p in pairs]), regs([p[0] for p in pairs]))
        for o, i in pairs:
            if add:
                h = g.dma_start(raw(o), raw(i), accum_op=op.add)
            elif slow:
                h = g.dma_start(raw(o), raw(i), allow_slow_non_contiguous=True)
            else:
                h = eng[e].dma_start(raw(o), raw(i))
            h.then_inc(T.sem[s], 16)
        count[s] = 16 * len(pairs)
        note(None, (s, count[s]), regs([p[1] for p in pairs]), regs([p[0] for p in pairs]))

    peers = [c for c in T.cores if c != core]
    peers.sort(key=lambda c: topo.die(c) == topo.die(core))
    lanes = (0, 2, 1)

    def exchange(src_of, dst, land, rsem, lsem):
        trs, reads, ne = [], [], 0
        for k, c in enumerate(peers):
            es = topo.engines(core, c)[lanes[k]::4]
            rid, pid, _ = topo.addr(c)
            s = src_of(T.rank_of(c))
            reads.append(s)
            ne += len(es)
            trs.append(RemoteDMATransfer(dst_ids=[DstId(rid=rid, pnc=pid)], dma_engine_mask=sum(1 << x for x in es),
                                         remote_sem=T.sem[rsem], src=s[0], dst=dst[0]))
        sync("G", None, regs(reads), [])
        g.remote_dma_fused(trs, local_sem=T.sem[lsem])
        count[lsem] = ne
        note(None, (lsem, ne), regs(reads), [])
        count[rsem] = sum(len(topo.engines(c, core)[0::4]) for c in peers)
        note(None, (rsem, count[rsem]), [], regs(land))

    def col(name, j):
        return A(name, j, j + 1)

    def ps(b, a=0, e=256, step=1):
        return A("ps%d" % b, a, e, step)

    FR = W
    H = W // 2
    NN_, PA_, SD_, HD_, IT_ = 0, 256, 512, 768, 832
    (CA, CB, CC, CK, CG, CIB, CEO, CEP, CPT, CX, CNAT, CTAU, CKA, CKB, CM1, C15, C120, C1, CPE,
     CO1, CP0, CP1, CDP, CGK, CT) = range(25)
    ES = 262144.0

    def rows(dst, r, a, src_off, wd=W, n=256):
        return [(A(dst, a, a + wd, row=r), A("HB", src_off, src_off + n)),
                (A(dst, a, a + wd, row=r + 8), A("LB", src_off, src_off + n))]

    def split_bits(a):
        ts(A("HI"), A("INI", a, a + 256), 4, op.logical_shift_right)
        ts(A("LO"), A("INI", a, a + 256), 15, op.bitwise_and)
        copy(A("HB", a, a + 256), A("HI"))
        copy(A("LB", a, a + 256), A("LO"))

    def split_round(a, n, src=None):
        src = src or A("INI", a, a + n)
        copy(A("HB", a, a + n), src)
        tt(A("LB", a, a + n), src, A("HB", a, a + n), op.subtract)

    sc_done = [0]

    def scatter(n):
        a = sc_done[0]
        n = min(n, W - a)
        if n > 0:
            off = A("SCO", a // 16, (a + n) // 16)
            src = A("WT", a, a + n)
            comp("V", lambda: g.vector.tensor_copy(IX(A("INV"), off)[0], src[0]), [A("INV")], [src], off[1])
            sc_done[0] = a + n

    def sign_v(src, a, b):
        ts(A("X0", a, b), src, 3.5, op.is_ge, 0.5, op.subtract)

    def sign_s(src, a, b):
        act(A("X0", a, b), src, fn.Sign, bias=col("CF", CX))

    dma("Y", [(A("INI", PA_, PA_ + 256), T.par[:]), (A("INI", SD_, SD_ + 256), T.side[:]),
              (A("INI", HD_, HD_ + 64), T.heads[:])])
    for k in range(4):
        dma("Y", [(A("UU", 1024 * k, 1024 * k + 1024), T.cnt[:, 1024 * k:1024 * k + 1024])])
    gz = P["gz"]
    iota(A("INI", NN_, NN_ + 256), [[1, 256]], 0, 256, False)
    iota(col("RI", 0), [[0, 1]], 0, 1, False)
    iota(A("IO16"), [[1, 16]], 0, 0)
    iota(A("ONE"), [[0, 128]], 1, 0)
    iota(A("Z1"), [[0, ZW]], 0, 0)
    asel(A("Z1", 15, 128, 16), A("ONE", 0, 8), [[-16, 8]], op.is_ge, 0, 1)
    asel(A("Z1", 15, 128, 16), A("Z1", 15, 128, 16), [[16, 8]], op.is_ge, 15, -1)
    iota(A("SEL", 0, 64), [[0, 64]], 0, 0)
    for h in range(2):
        asel(A("RT", 64 * h, 64 * h + 64), A("ONE", 0, 64), [[-2, 64]], op.is_equal, -h, 1)
    asel(A("IDN"), A("ONE"), [[-1, 128]], op.is_equal, 0, 1)
    iota(A("NI4"), [[16, 256]], W, 0)
    iota(A("WT", 0, gz), [[0, gz]], 0, 0)
    iota(A("INV", 0, W), [[0, W]], 0, 0)
    dma("G", [(col("THI", 0), T.th[:])], slow=True)
    asel(A("BO"), A("ONE"), [[-16, 8], [0, 16]], op.is_ge, 0, 1)
    asel(A("BO"), A("BO"), [[16, 8], [0, 16]], op.is_ge, 15, -1)
    iota(A("NHI"), [[1, 256]], 0, 0)
    iota(A("Z0"), [[0, 128]], 0, 0)
    iota(A("REPF"), [[0, W]], 0, 0)

    memset(A("WT", FR, FR + W), 1.0)
    for c, v in ((CX, -3.5), (CM1, -1.0), (C1, 1.0)):
        memset(col("CF", c), v)
    ts(A("INI", NN_, NN_ + 256), A("INI", NN_, NN_ + 256), W - 1, op.bitwise_and)
    split_bits(NN_)
    dma("S", rows("WT", 1, FR, NN_) + rows("WT", 3, FR, NN_))
    memset(A("GI1"), 0.0)
    split_bits(PA_)
    split_round(SD_, 320)
    dma("Y", rows("GI1", 0, 0, HD_, NI, 64))
    dma("Y", rows("WT", 2, FR, SD_) + rows("WT", 0, FR, PA_))
    if gz < W:
        memset(A("WT", gz, W), 0.0)
    ts(col("RJ", 0), col("RI", 0), 15, op.bitwise_and)
    ts(col("RJ", 1), col("RI", 0), 7, op.bitwise_and)
    copy(A("RF", 0, 2), A("RJ", 0, 2))
    ts(A("OH"), A("IO16"), col("RF", 0), op.is_equal)
    ts(A("OP"), A("IO16", 0, 8), col("RF", 1), op.is_equal)
    ts(col("CF", CNAT), col("RF", 0), 8.0, op.is_lt, 15.0, op.mult)
    ts(col("CF", CTAU), col("RF", 0), 8.0, op.is_ge, 255.0, op.mult)
    ts(A("CF", CNAT, CTAU + 1), A("CF", CNAT, CTAU + 1), 1.0, op.add)
    ts(A("PN"), A("OP"), col("CF", CNAT), op.mult)
    ts(A("PU"), A("OP"), col("CF", CTAU), op.mult)
    ts(col("CF", CA), col("OH", 14), 8192.0, op.mult, col("PN", 0), op.add)
    ts(col("CF", CB), col("OP", 2), col("PN", 1), op.subtract)
    ts(col("CF", CC), col("OH", 14), -8192.0, op.mult, col("PN", 3), op.add)
    memset(A("NX", 0, 8), 0.0)

    def late_consts():
        ts(col("CF", CK), col("PN", 1), col("PN", 2), op.add)
        ts(col("CF", CIB), col("OH", 6), 1024.0, op.mult, col("OP", 5), op.add)
        ts(col("CF", CPT), col("PU", 0), col("PU", 3), op.add)
        ts(col("CF", CPE), col("OH", 6), 0.25, op.mult, col("OH", 7), op.add)
        ts(col("CF", CKA), col("OP", 2), col("OP", 3), op.add, col("OP", 0), op.subtract)
        ts(col("CF", CPE), col("CF", CPE), 0.125, op.mult)
        ts(col("CF", CKA), col("CF", CKA), col("OP", 1), op.subtract, col("OH", 7), op.subtract)
        ts(col("CF", CEO), col("CF", CPE), col("CF", CPT), op.add, ES, op.mult)
        ts(col("CF", CEP), col("CF", CPE), col("CF", CPT), op.subtract, ES, op.mult)
        ts(col("CF", CKA), col("CF", CKA), col("OH", 14), op.subtract, col("OH", 15), op.subtract)
        ts(col("CF", CDP), col("OH", 15), 4096.0, op.mult)
        ts(col("CF", CT), col("OH", 15), 0.5, op.mult, col("OH", 14), op.add)
        ts(col("CF", CO1), col("OH", 13), ES / 8, op.mult, col("CF", CEO), op.add)
        ts(col("CF", CP1), col("OH", 13), ES / 8, op.mult, col("CF", CEP), op.add)
        ts(col("CF", CP0), col("CF", CT), 4096.0, op.mult, col("CF", CEP), op.add)
        ts(col("CF", CT), col("OH", 15), 0.5, op.mult, col("OH", 14), op.subtract)
        ts(col("CF", CGK), col("OP", 0), col("OP", 1), op.add, col("OP", 2), op.add)
        ts(col("CF", CKB), col("CF", CKA), 8.5, op.mult)
        ts(col("CF", CP1), col("CF", CT), 4096.0, op.mult, col("CF", CP1), op.add)
        ts(col("CF", CGK), col("CF", CGK), col("OP", 3), op.add)
        ts(col("CF", CG), col("OP", 5), -1.0, op.mult)
        for c, v in ((C15, 15.0), (C120, 120.0)):
            memset(col("CF", c), v)
        for kb in ("K0", "K1"):
            memset(A(kb, 0, 16), 0.0)
            memset(A(kb, NI + 16, NI + 32), 0.0)
        memset(A("UU", 2 * W, 2 * W + 16), 0.0)
        memset(A("TT", 2 * W, 2 * W + 16), 0.0)

    zcol = {"HD": col("OP", 0), "PAR": col("PN", 0), "C": col("CF", CC), "SD": col("OP", 2), "IT": col("OP", 5),
            "IB": col("CF", CIB), "K": col("CF", CK), "U": col("CF", CDP), "EO0": col("CF", CEO), "EO1": col("CF", CO1),
            "EP0": col("CF", CP0), "EP1": col("CF", CP1), "IV": col("PU", 3), "PT": col("CF", CPT)}

    def zmake(names):
        for z in names:
            o = ZN.index(z) * ZW
            act(A("ZS", o, o + ZW), A("Z1"), fn.Copy, scale=zcol[z])

    for k in range(0, W, 1024):
        sign_s(A("UU", k, k + 1024), k, k + 1024)
        block(ps(7), "ONE", "X0", k // 256, k // 256 + 4, k == 0, k == W - 1024)
    act(A("VB"), ps(7), fn.Relu, bias=col("CF", C1), scale=col("CF", CM1))
    dma("S", [(A("WT", FR, FR + W, row=14), A("VB"))])
    zmake(["HD"])
    wrap(ps(1, 0, 64), "HD", "GI1", 0, NI)
    for j, c in ((0, col("OP", 2)), (16, col("CF", CA)), (32, col("CF", CB)), (48, col("CF", CA))):
        act(A("SEL", j, j + 16, 2), A("Z1", 15, 128, 16), fn.Copy, scale=c)
    act(A("RF32"), A("RT"))
    zmake(["C", "PAR", "SD"])
    act(A("IDF"), A("IDN"))
    act(A("NID"), A("IDN"), fn.Copy, scale=col("CF", CM1))
    dma("Y", rows("WT", 0, 0, PA_) + rows("WT", 3, 0, NN_) + [(A("WT", 0, W, row=14), A("VB"))])
    dma("Y", [(A("INI", IT_, IT_ + 256), T.itm[:]), (A("BI"), T.bit[:])])
    late_consts()
    ts(A("NI4"), A("NI4"), col("RF", 0), op.add)
    ts(A("FA"), A("INI", SD_, SD_ + 256), 0.0, op.is_equal)
    tt(A("FA"), A("FA"), A("NI4"), op.mult)
    tt(A("FA"), A("FA"), A("INI", SD_, SD_ + 256), op.add)
    copy(A("OFF0"), ps(1, 0, 64))
    copy(A("SCO"), A("FA"))
    zmake(["IT", "IB", "K", "U", "EO0", "EO1", "EP0", "EP1", "IV", "PT"])
    for j, c in ((64, col("CF", CEO)), (72, col("CF", CG)), (80, col("CF", CEP)), (88, col("OP", 4))):
        act(A("SEL", j, j + 8), A("Z1", 15, 128, 16), fn.Copy, scale=c)

    def extras_a(t, s):
        if t == 0:
            if s == 1:
                copy(A("HB", IT_, IT_ + 256), A("INI", IT_, IT_ + 256))
            if s == 2:
                copy(A("BITB"), A("BI"))
            if s == 3:
                ts(A("BROW"), A("BITB"), -0.5, op.add)
                ts(col("BROW", 0), col("OH", 0), 4.0, op.mult, col("BROW", 0), op.add)
            if s == 4:
                tt(A("SB2", 0, 256), A("HB", SD_, SD_ + 256), A("BITB"), op.mult)
            if s == 5:
                tt(A("SB2", 256, 512), A("LB", SD_, SD_ + 256), A("BITB"), op.mult)
            if s == 6:
                ts(A("NW"), A("NI4"), float(W), op.subtract)
                copy(col("THF", 0), col("THI", 0))
            if s >= 2:
                scatter(P["sc_a"])
        else:
            if s == 2:
                ts(A("ITI1"), A("XI"), -496.0, op.add, 1040.0, op.min)

    def extras_b(t, s):
        if t == 0:
            if s == 1:
                tt(A("LB", IT_, IT_ + 256), A("INI", IT_, IT_ + 256), A("HB", IT_, IT_ + 256), op.subtract)
            elif 2 <= s < STEPS - 1:
                scatter(P["sc_b"])
        else:
            if s == 0:
                copy(A("PARI"), ps(6))
            if s == 1:
                tt(A("SA1"), A("SIDE"), A("SA0"), op.subtract)
            if s == 2:
                tt(A("RBF"), A("NV"), A("NW"), op.subtract)
            if s == 3:
                tt(A("NV"), A("NV"), A("BV"), op.subtract)
            if s == 4:
                tt(A("FA"), A("SA1"), A("NV"), op.add)
            if s == 5:
                copy(A("PT1"), A("FA"))

    for t in range(ROUNDS):
        last = t == ROUNDS - 1
        KB, LB_ = "K%d" % t, "LAND%d" % t
        US, UD = ("UU", "TT") if t == 0 else ("TT", "UU")
        iv, uv = P["iv"], P["uv"][t]
        parts = [(uv, 512, 3), (512, NI, 4)] + ([(0, uv, 5)] if last and uv else [])

        def counts(s):
            gu = "GU%d" % (s % 2)
            copy(A("OC", 64 * s, 64 * s + 64), ps(2, 0, 64))
            m = 512 if s == STEPS - 1 else uv

            def ix(a, b):
                return IX(A(US, 0, W), A("OC", 64 * s + a // 16, 64 * s + b // 16))
            if last:
                if m:
                    ts(A(gu, 0, m), ix(0, m), 15.0, op.min)
                act(A(gu, m, NI), ix(m, NI), fn.Relu, bias=col("CF", C15), scale=col("CF", CM1))
            else:
                if uv and s == 0:
                    copy(A("ACC", 0, uv), ix(0, uv))
                elif uv:
                    tt(A("ACC", 0, uv), ix(0, uv), A("ACC", 0, uv), op.add)
                act(A(gu, m, NI), ix(m, NI))
                if m > uv:
                    copy(A(gu, uv, m), ix(uv, m))

        def counts_add(s):
            for a, b, bank in parts:
                neg = last and (a >= 512 or (a >= uv and s < STEPS - 1))
                mms(ps(bank, 0, b - a), [(A("NID" if neg else "IDN"), A("GU%d" % (s % 2), a, b))], s == 0, s == STEPS - 1)

        for s in range(STEPS):
            gi = "GI%d" % (s % 2)
            on, oo, win = ("OFF0", 0, A("WT", FR, FR + W)) if s == 0 else ("OFF", 64 * s, A("WT"))
            copy(A(gi, 0, iv), IX(win, A(on, oo, oo + iv // 16)))
            act(A(gi, iv, NI), IX(win, A(on, oo + iv // 16, oo + 64)))
            if s == STEPS - 1 and t == 0:
                dma("Y", rows("WT", 5, FR, IT_) + [(A("WT", FR, FR + W, row=6), A("BROW"))])
            if s > 0:
                counts(s - 1)
            extras_a(t, s)
            if s < STEPS - 1:
                so = 0 if s == 0 else 32
                mmx([(ps(0, ch, 256, 8), A(gi, ch, NI, 8), A("SEL", so, so + 32), True, True) for ch in range(8)])
                if s == 0:
                    ts(A("Q"), ps(0, 0, 128), float(W), op.add)
                else:
                    tt(A("Q"), ps(0, 0, 128), A("Q"), op.add)
                tt(A("NX", 8, 136), ps(0, 128, 256), A("Q"), op.min)
                mms(ps(1, 0, 64), [(A("NX", 8, 136), A("RF32", 0, 64)), (A("NX", 0, 128), A("RF32", 64, 128))], True, True)
            wrap(ps(2, 0, 64), "C", gi, 0, NI)
            if s > 0:
                counts_add(s - 1)
            extras_b(t, s)
            if s < STEPS - 1:
                copy(A("OFF", 64 * s + 64, 64 * s + 128), ps(1, 0, 64))
        counts(STEPS - 1)
        counts_add(STEPS - 1)
        for a, b, bank in parts:
            o, i = A("ACC", a, b), ps(bank, 0, b - a)
            if a >= 512:
                if last:
                    act(o, i, fn.Identity, bias=col("CF", C120))
                else:
                    act(o, i)
            elif last and a >= uv:
                ts(o, i, 105.0, op.add)
            else:
                copy(o, i)

        exchange(lambda r: A("ACC", OWN * r, OWN * r + OWN), A(LB_, OWN * rank, OWN * rank + OWN),
                 [A(LB_, OWN * T.rank_of(c), OWN * T.rank_of(c) + OWN) for c in peers], "la%d" % t, "l%d" % (2 * t))
        vpre = P["vpre"] if last else 0

        def above(k):
            o, i = A("PPB", k, k + 1024), IX(A("WT", FR, FR + W), A("PARI", k // 16, k // 16 + 64))
            if k < vpre:
                copy(o, i)
            else:
                act(o, i)

        def above_list(k):
            wrap(ps(2 + k // H, k % H // 16, k % H // 16 + 64), "IT", "PPB", k, k + 1024)
            dma("Y", [(A("PPB", k, k + 1024, row=2, rs=8), A("WT", FR + k, FR + k + 1024, row=1, rs=8)),
                      (A("PPB", k, k + 1024, row=14), A("WT", FR + k, FR + k + 1024, row=6))])

        def summed(k, e):
            o, i = A(US, W + k, W + k + 1024), IX(A(US, 0, W), A("PARI", k // 16, k // 16 + 64))
            if e == "V":
                copy(o, i)
            else:
                act(o, i)

        def summed_add(k):
            dma("G", [(A(US, W + k, W + k + 1024), A(US, k, k + 1024))], add=True)

        if t == 0:
            for k in range(0, W, 1024):
                wrap(ps(5 + k // 1024 % 2, 0, 64), "PAR", "WT", k, k + 1024)
                copy(A("PARI", k // 16, k // 16 + 64), ps(5 + k // 1024 % 2, 0, 64))
                above(k)
                scatter(P["sc_h0"])
            wrap(ps(7), "IB", "WT", FR, FR + W)
            scatter(W)
        else:
            for k in range(0, W, 1024):
                above(k)
        for k, e in P["sum1"][t]:
            summed(k, e)
        above_list(0)
        above_list(1024)
        if t == 0:
            wrap(ps(5), "SD", "WT", FR, FR + W)
        srcs = [A("ACC", OWN * rank, OWN * rank + OWN)] + [A(LB_, OWN * T.rank_of(c), OWN * T.rank_of(c) + OWN) for c in peers]
        mms(ps(0, 0, OWN), [(A("IDN"), x) for x in srcs], True, True)
        ts(A("VI"), ps(0, 0, OWN), col("THF", 0), op.is_ge)
        mms(ps(1, 0, OWN), [(A("BO"), A("VI"))], True, True)
        mine = A(KB, 16 + OWN * rank, 16 + OWN * rank + OWN)
        ts(mine, ps(1, 0, OWN), col("CF", CKA), op.mult, col("CF", CKB), op.is_gt)
        exchange(lambda r: mine, mine, [A(KB, 16 + OWN * T.rank_of(c), 16 + OWN * T.rank_of(c) + OWN) for c in peers],
                 "ka%d" % t, "l%d" % (2 * t + 1))
        if t == 0:
            wrap(ps(4), "IV", "INV", 0, W)
        above_list(2048)
        above_list(3072)
        act(A("YA", OWN * t, OWN * t + OWN), ps(0, 0, OWN))
        dma("Y", [(T.ya[:, OWN * t:OWN * t + OWN], A("YA", OWN * t, OWN * t + OWN))])
        ts(A("IPO", 0, 128), ps(2, 0, 128), 16.0, op.add)
        for k, e in P["sum2"][t]:
            summed(k, e)
        for k in range(0, W, 1024):
            summed_add(k)
        if t == 0:
            ts(A("ITI0"), ps(7), 528.0, op.add, 1040.0, op.min)
            ts(A("BIF"), ps(7), 512.0, op.is_ge)
            ts(A("NBF"), ps(7), 512.0, op.is_lt)
            act(A("XI"), ps(7))
            tt(A("SA0"), ps(5), A("NBF"), op.mult)
            act(A("SIDE"), ps(5))
            tt(A("BV"), ps(4), A("BIF"), op.mult)
            copy(A("IVI"), ps(4))
            act(A("NV"), ps(4))
            tt(A("FA"), A("SA0"), A("BV"), op.add)
            copy(A("PT0"), A("FA"))
            ts(A("HI"), A("IVI"), 4, op.logical_shift_right)
            ts(A("LO"), A("IVI"), 15, op.bitwise_and)
            tt(A("RB2", 0, 256), A("HI"), A("NHI"), op.subtract)
            ts(A("RB2", 256, 512), A("LO"), col("RF", 0), op.subtract)
        ts(A("IPO", 128, 256), ps(3, 0, 128), 16.0, op.add)

        Q4 = range(4)

        def qs(q):
            return 1024 * q, 1024 * q + 1024

        def take(name, q):
            copy(A(name, 64 * q, 64 * q + 64), ps(q, 0, 64))

        for q in Q4:
            a0, b0 = qs(q)
            tt(A("X0", a0, b0), IX(A(KB), A("IPO", 64 * q, 64 * q + 64)), A("PPB", a0, b0), op.mult)
            if q:
                take("JO0", q - 1)
            wrap(ps(q, 0, 64), "K", "X0", a0, b0)
            if q % 2:
                a0 -= 1024
                act(A("KN", a0, b0), IX(A(KB), A("ITI%d" % t, a0 // 16, b0 // 16)), fn.Copy, scale=col("OH", 7))
                st = [(A("KN", a0, b0, row=6), A("WT", FR + a0, FR + b0, row=6)),
                      (A("KN", a0, b0, row=14), A("X0", a0, b0, row=14)), (A("KN", a0, b0, row=15), A("X0", a0, b0, row=15))]
                if not last:
                    st.append((A("KN", a0, b0, row=5, rs=8), A("WT", FR + a0, FR + b0, row=2, rs=8)))
                dma("Y", st)
            if q == 1:
                wrap(ps(4, 0, 128), "U", "X0", 0, H, more=[(A("IDF"), A("NW", 0, 128))])
        if last:
            dma("Y", [(A("KN", row=13), A("AB"))])
        else:
            dma("Y", [(A("KN", row=4), A("SB2", 0, 256)), (A("KN", row=12), A("SB2", 256, 512))])
        chain = ["X0", "J2", "J4"]
        for lv in range(2):
            src, dst = chain[lv], chain[lv + 1]
            oi, on = "JO%d" % lv, "JO%d" % (lv + 1)
            a = P["lv"]
            for q in Q4:
                c0 = 64 * q
                vo, vi_ = A(dst, 16 * c0, 16 * (c0 + a)), IX(A(src), A(oi, c0, c0 + a))
                so, si = A(dst, 16 * (c0 + a), 16 * (c0 + 64)), IX(A(src), A(oi, c0 + a, c0 + 64))
                if lv:
                    ts(vo, vi_, col("CF", CGK), op.mult)
                    act(so, si, fn.Copy, scale=col("CF", CGK))
                else:
                    copy(vo, vi_)
                    act(so, si)
                if q == 0 and lv == 0:
                    take(oi, 3)
                elif q == 1 and lv == 0:
                    copy(A("UL", 0, 128), ps(4, 0, 128))
                elif q < 2:
                    take(oi, q + 2)
                if q >= 2:
                    take(on, q - 2)
                wrap(ps(q, 0, 64), "K", dst, 1024 * q, 1024 * q + 1024)
        wrap(ps(4, 128, 256), "U", "X0", H, W, more=[(A("IDF"), A("NW", 128, 256))])

        def dropped(a0, b0):
            act(A("U1", a0, b0), IX(A(US), A("UL", a0 // 16, b0 // 16)))

        dropped(0, H)
        XB = 5
        SA, PT = "SA%d" % t, "PT%d" % t

        def own_list(w):
            wrap(ps(w, 0, 128), "PT", "P1", H * w, H * w + H)

        def own_take(w):
            copy(A("P1O", 128 * w, 128 * w + 128), ps(w, 0, 128))

        def turned(src, so, c0, c1, stop=False):
            mmx([(ps(XB, 256 * (ch % 2) + ch // 2, 256 * (ch % 2) + 256, 16), A(src, 128 * ch, 128 * ch + 128),
                  A("SEL", so, so + 16), False, stop and ch == c1 - 1) for ch in range(c0, c1)])

        if not last:
            mms(ps(XB, 0, 512), [(A("Z0"), A("X0", 0, 512))], True, False)
        for q in Q4:
            a0, b0 = qs(q)
            tt(A("P1", a0, b0), IX(A("J4"), A("JO2", a0 // 16, b0 // 16)), A("KN", a0, b0), op.add)
            if q < 2:
                take("JO2", q + 2)
            if q == 1:
                copy(A("UL", 128, 256), ps(4, 128, 256))
                dropped(H, W)
            wrap(ps(q, 0, 64), "EO%d" % t, "P1", a0, b0, True, False)
            if not last and q < 3:
                turned("P1", 64, 8 * q, 8 * q + 8)

        def decide(q):
            c0 = 64 * q
            ts(A("GO", c0, c0 + 64), ps(q, 0, 64), float(2 * W), op.min)
            ts(A("MW", c0, c0 + 64), ps(q, 0, 64), 0.0, op.is_equal)

        a = P["ppv"]
        for q in Q4:
            c0 = 64 * q
            copy(A("PP", 16 * c0, 16 * (c0 + a[q])), IX(A("P1"), A(PT, c0, c0 + a[q])))
            act(A("PP", 16 * (c0 + a[q]), 16 * (c0 + 64)), IX(A("P1"), A(PT, c0 + a[q], c0 + 64)))
            if q >= 2:
                decide(q - 2)
            wrap(ps(q, 0, 64), "EP%d" % t, "PP", 1024 * q, 1024 * q + 1024, False, True, more=[(A("IDF"), A(SA, c0, c0 + 64))])

        def absorb_v(a0, b0):
            tt(A(UD, a0, b0), IX(A(US), A("GO", a0 // 16, b0 // 16)), A("U1", a0, b0), op.add)

        def counts_out(a0, b0):
            dma("Y", [(T.yc[:, a0:b0], A("UU", a0, b0))])

        RW, PO_ = ("REPF", "PAO") if last else ("J2", "J4")

        def parents(e, a0, b0):
            o, i = A(PO_, a0, b0), IX(A(RW), A("P1O", a0 // 16, b0 // 16))
            if e == "S":
                act(o, i)
            else:
                copy(o, i)
            if last:
                dma("Y", [(T.yp[:, a0:b0], A("PAO", a0, b0, row=0))])
            else:
                dma("Y", [(A("WT", FR + a0, FR + b0, row=0, rs=8), A("J4", a0, b0, row=0, rs=8))])

        pav, sa = P["pav"][t], P["abs_"][t]
        if last:
            for j in range(0, sa, 512):
                act(A("GI0", j, j + 512), IX(A(US), A("GO", j // 16, j // 16 + 32)))
            decide(2)
            if P["early"]:
                absorb_v(sa, sa + P["early"])
            decide(3)
            tt(A("WF"), A("MW"), A("RBF"), op.mult)
            tt(A("WF"), A("WF"), A("NW"), op.add)
            dma("Y", [(A("REPF", row=0), A("WF"))])
            own_list(0)
            for j in range(0, sa, 512):
                mms(ps(4 + j // 512, 0, 512), [(A("IDN"), A("U1", j, j + 512)), (A("IDN"), A("GI0", j, j + 512))], True, True)
            own_list(1)
            for a0 in range(sa, W, 1024):
                b0 = min(a0 + 1024, W)
                if a0 == sa + 1024:
                    own_take(1)
                absorb_v(a0 + (P["early"] if a0 == sa else 0), b0)
                ts(A("UU", a0, b0), A("UU", a0, b0), 15.0, op.min)
                counts_out(a0, b0)
                if a0 == sa:
                    own_take(0)
                    for j in range(0, sa, 512):
                        ts(A("UU", j, j + 512), ps(4 + j // 512, 0, 512), 15.0, op.min)
                    if sa:
                        counts_out(0, sa)
        else:
            for j in range(0, sa, 1024):
                act(A("TT", j, j + 1024), IX(A(US), A("GO", j // 16, j // 16 + 64)))
                dma("G", [(A("TT", j, j + 1024), A("U1", j, j + 1024))], add=True)
            decide(2)
            if P["early"]:
                absorb_v(sa, sa + P["early"])
            decide(3)
            tt(A("W2", 0, 256), A("MW"), A("RB2", 0, 256), op.mult)
            tt(A("W2", 256, 512), A("MW"), A("RB2", 256, 512), op.mult)
            tt(A("W2", 0, 256), A("W2", 0, 256), A("NHI"), op.add)
            ts(A("W2", 256, 512), A("W2", 256, 512), col("RF", 0), op.add)
            dma("Y", [(A("J2", row=0), A("W2", 0, 256)), (A("J2", row=8), A("W2", 256, 512))])
            turned("P1", 64, 24, 32)
            turned("PP", 80, 0, 32, True)
            own_list(0)
            order = list(range(sa, W, 1024)) + list(range(0, sa, 1024))
            for n, k in enumerate(order):
                if k >= sa:
                    absorb_v(k + (P["early"] if k == sa else 0), k + 1024)
                if n == 0:
                    for h in range(2):
                        ts(A("M", 128 * h, 128 * h + 128), ps(XB, 256 * h, 256 * h + 128), 0.0, op.is_equal)
                        tt(A("FD", 128 * h, 128 * h + 128), ps(XB, 256 * h + 128, 256 * h + 256), A("M", 128 * h, 128 * h + 128), op.mult)
                    mmx([(ps(4), A("IDN"), A("HB", SD_, SD_ + 256), True, False), (ps(4), A("IDN"), A("LB", SD_, SD_ + 256), False, False),
                         (ps(4, 0, 128), A("FD", 0, 128), A("IDF"), False, False), (ps(4, 128, 256), A("FD", 128, 256), A("IDF"), False, True)])
                    mmx([(ps(6, 128 * h, 128 * h + 128), A("M", 128 * h, 128 * h + 128), A("IDN"), True, True) for h in range(2)])
                    own_list(1)
                    own_take(0)
                if n == 1:
                    split_round(SD_, 256, ps(4))
                    dma("Y", rows("WT", 2, FR, SD_))
                    own_take(1)
                if n in P["sgv"]:
                    sign_v(A("TT", k, k + 1024), k, k + 1024)
                else:
                    sign_s(A("TT", k, k + 1024), k, k + 1024)
                block(ps(7), "ONE", "X0", k // 256, k // 256 + 4, n == 0, n == 3)
        cuts = [c for c in (0, 1024, H, W - 1024, W) if c <= W - pav]
        for a0, b0 in zip(cuts[:-1], cuts[1:]):
            parents("S", a0, b0)
        for a0 in range(W - pav, W, 1024):
            parents("V", a0, min(a0 + 1024, W))
        if not last:
            ts(A("VB"), ps(7), 0.25, op.is_lt)
            dma("S", [(A("WT", FR, FR + W, row=14), A("VB"))])
            tt(A("AB"), ps(6), A("BITB"), op.mult)
            wrap(ps(6), "PAR", "J4", 0, W)
            dma("Y", [(A("WT", 0, W, row=0, rs=8), A("J4", row=0, rs=8)), (A("WT", 0, W, row=14), A("VB"))])

    for s in sorted(count):
        if not any(waited[e].get(s, 0) >= count[s] for e in eng):
            wait("Y", s, count[s])
